import numpy as np, ml_dtypes
CORES = [16,18,20,22]
N = 4
BF = ml_dtypes.bfloat16
W, WX, I, B, SH = 4096, 4096, 256, 16, 12
DR, IR, GAP, RO = 6, 12, 4, 4
def parts(rng):
    mid = rng.choice(np.array([0.02, 0.05, 0.15, 0.4]), (N, 8, 1, 1)); e = rng.integers(0, 16, (N, 8, 16, WX)); small = (e * 5) >> 4
    x = np.where(rng.random((N, 8, 1, WX)) < mid, e, np.where(rng.random((N, 8, 1, WX)) < 0.5, small, 11 + small))
    g = np.minimum(np.maximum(rng.integers(1, 10, (N, 8, 1, I)) + rng.integers(-2, 3, (N, 8, 16, I)), 0), 15)
    g = np.where(rng.random((N, 8, 1, I)) < 0.1, rng.integers(0, 16, g.shape), g)
    return x, g, rng.integers(0, W * WX, (N, 8, 16, W)), rng.integers(0, W, (N, 8, 16, I)), rng.integers(0, WX, (N, 8, 16, I))
def pack(x, g, rel, nam, grd):
    return {"xc": np.ascontiguousarray(x.reshape(N, 128, WX)).astype(np.float32).astype(BF), "rel": np.ascontiguousarray(rel.reshape(N, 128, W)).astype(np.int32),
            "nam": np.ascontiguousarray(nam.reshape(N, 128, I)).astype(np.int32), "grd": np.ascontiguousarray(grd.reshape(N, 128, I)).astype(np.int32),
            "lim": np.ascontiguousarray(g.reshape(N, 128, I)).astype(np.float32).astype(BF)}
def setup_inputs(rng):
    return pack(*parts(rng))
def skew(rng, n, shape):
    ex = rng.choice(np.array([1, 3, 6], np.float32), (N, 8, 1, 1))
    return np.minimum((n * rng.random(shape, dtype=np.float32) ** ex).astype(np.int64), n - 1)
def setup_inputs_spread(rng):
    x = np.minimum((16 * rng.random((N, 8, 1, WX), dtype=np.float32) * rng.random((N, 8, 16, WX), dtype=np.float32)).astype(np.int64), 15)
    x = np.where(rng.random((N, 8, 1, WX)) < 0.5, 15 - x, x)
    g = np.minimum((16 * rng.random((N, 8, 1, I)) * rng.random((N, 8, 16, I))).astype(np.int64), 15)
    return pack(x, g, skew(rng, W, (N, 8, 16, W)) + W * skew(rng, WX, (N, 8, 16, W)), skew(rng, W, (N, 8, 16, I)), skew(rng, WX, (N, 8, 16, I)))
def atends(rng, hi, shape, share):
    u = rng.random(shape)
    return np.where(u < 0.5 * share, 0, np.where(u < share, hi, rng.integers(0, hi + 1, shape)))
def kinds(rng, n):
    m = rng.random((N, 8, 1, n)); e = rng.integers(0, 2, (N, 8, 16, n))
    return 15 * np.where(m < 0.25, 0, np.where(m < 0.5, 1, e))
def setup_inputs_ends(rng):
    x = kinds(rng, WX); g = kinds(rng, I); big = W * WX - 1
    u = rng.random((N, 8, 16, W)); two = rng.integers(0, 2, u.shape)
    rel = np.where(u < 0.35, 0, np.where(u < 0.7, big, np.where(u < 0.85, np.where(two == 1, W - 1, W * (WX - 1)), rng.integers(0, W * WX, u.shape))))
    nam = atends(rng, W - 1, (N, 8, 16, I), 0.75); grd = atends(rng, WX - 1, (N, 8, 16, I), 0.75)
    for c in (0, WX - 1):
        x[:, :, :, c] = 15 * rng.integers(0, 2, (N, 8, 16)); x[0, :, :, c] = 0; x[1, :, :, c] = 15; x[N - 1, :, :, c] = 15
    for q in (0, 1, N - 1): grd[q] = (WX - 1) * rng.integers(0, 2, (8, 16, I))
    for q in (1, N - 1):
        turn = (np.arange(16)[None, :, None] + rng.integers(0, 16, (8, 1, I))) & 15
        g[q] = np.where(turn < 8, 0, g[q]); g[q, 7, :, I - 1] = 0; g[q, 0, :, 0] = 0; g[q, 3, :8, I - 1] = 0; g[q, 3, 8:, I - 1] = 15
    for q in range(N):
        if 1 < q < N - 1 or q == 0: g[q, :, :, 0] = 15; g[q, :, :, I - 1] = 15; g[q, :, :, 1] = 0; g[q, :, :, I - 2] = 0
    x[1, 7, :, WX // 2] = 0; grd[1, 7, 15, I - 1] = WX // 2
    for q in range(N):
        rel[q, 7, 15, W - 1] = big; rel[q, 0, 0, 0] = big; rel[q, 7, 15, 0] = 0; nam[q, 0, 0, 0] = 0; nam[q, 7, 15, I - 1] = W - 1; nam[q, 7, 0, I - 1] = W - 1
    return pack(x, g, rel, nam, grd)
def setup_inputs_corners(rng):
    x, g, rel, nam, grd = parts(rng)
    g = rng.integers(0, 15 - GAP, (N, 8, 16, I)); ones = np.arange(16)[:, None]
    ty = np.array([(16, 0), (0, 16), (0, 0), (DR, 16 - DR), (DR - 1, 17 - DR), (0, IR - 1), (0, IR), (DR + 1, 0), (16 - IR, IR), (17 - IR, IR - 1), (DR, 0), (DR - 1, 0)])
    c = np.arange(WX) & (B - 1); which = np.where(c < 8, c, rng.integers(0, 12, (N, 8, WX)))
    over = ty[which, 0][:, :, None, :]; under = ty[which, 1][:, :, None, :]
    role = (ones * (2 * rng.integers(0, 8, (N, 8, 1, WX)) + 1) + rng.integers(0, 16, (N, 8, 1, WX))) & 15
    gg = np.repeat(g, B, axis=3); coin = rng.random(gg.shape) < 0.5
    v = np.where(role < over, np.where(coin, gg + GAP + 1, 15), np.where(role >= 16 - under, np.where(coin, gg, 0), np.where(coin, gg + 1, gg + GAP)))
    ca = (np.arange(I) + rng.integers(0, 10, (N, 8, 1, 1))) % 10; r = rng.integers(0, B, (N, 8, 16, I)); two = rng.integers(0, 2, (N, 8, 16, I))
    cs = np.where(ca == 1, 0, np.where(ca == 2, 1, np.where(ca == 3, 2, r)))
    cs = np.where(ca == 4, np.where(ones == 15, 2, 0), np.where(ca == 5, np.where(ones == 0, 2, two), cs))
    cs = np.where(ca == 6, 3 + (r & 3), np.where(ca == 7, two, np.where(ca == 8, np.where(ones == 15, 0, 1), cs)))
    col = B * np.arange(I) + cs
    for q in range(N):
        for w in range(8):
            o = rng.permutation(WX); x[q, w][:, o] = v[q, w]; grd[q, w] = o[col[q, w]]
    g = np.where(ca == 9, 15, g)
    l = np.arange(W); m = rng.integers(0, 5, rel.shape)
    rel = np.where(m == 0, l + W * np.minimum(l, WX - 1), np.where(m == 1, l + W * (rel >> SH), np.where(m == 2, (W - 1) * rng.integers(0, 2, rel.shape) + W * (WX - 1) * rng.integers(0, 2, rel.shape), rel)))
    nam = np.where(rng.random(nam.shape) < 0.3, (W - 1) * rng.integers(0, 2, nam.shape), nam)
    return pack(x, g, rel, nam, grd)
def setup_inputs_alike(rng):
    x, g, rel, nam, grd = parts(rng)
    grd[:, ::2] = rng.choice(np.array([0, WX - 1, WX // 2, 3]), (N, 4, 16, I)); grd[:, 1] = np.repeat(grd[:, 1, :1], 16, axis=1)
    nam[:, 2] = rng.choice(np.array([0, W - 1]), (N, 16, I)); nam[:, 3] = np.repeat(nam[:, 3, :1], 16, axis=1)
    rel[:, 5] = rng.choice(rng.integers(0, W * WX, 6), (N, 16, W)); rel[:, 7] = np.repeat(rel[:, 7, :1], 16, axis=1)
    x[:, 4] = 4 + GAP + rng.integers(0, 2, (N, 16, WX)); g[:, 4] = rng.choice(np.array([4, 4 + GAP]), (N, 16, I))
    x[N - 1, 4] = rng.integers(5, 5 + GAP, (16, WX)); g[N - 1, 4] = 4
    for q in range(N):
        c = int(rng.choice(np.array([0, WX - 1, WX // 2, 3]))); grd[q, 6] = c; x[q, 6, :, c] = rng.permutation(16)
        grd[q, 7] = rng.permutation(np.arange(16 * I) % WX).reshape(16, I)
    return pack(x, g, rel, nam, grd)
def check_inputs(d):
    bad = []
    for k, hi in (("xc", 15), ("rel", W * WX - 1), ("nam", W - 1), ("grd", WX - 1), ("lim", 15)):
        v = np.asarray(d[k]).astype(np.float64)
        if not (np.min(v) >= 0 and np.max(v) <= hi): bad.append("range of " + k)
        elif np.any(v != np.floor(v)): bad.append("whole numbers of " + k)
    return bad
def reference(xc, rel, nam, grd, lim):
    x = xc.astype(np.float32).astype(np.int32).reshape(N, 8, 16, WX); g = lim.astype(np.float32).astype(np.int32).reshape(N, 8, 16, I)
    tab = rel.reshape(N, 8, 16, W); a = nam.astype(np.int32).reshape(N, 8, 16, I); b = grd.astype(np.int32).reshape(N, 8, 16, I)
    deaths = np.zeros(N, np.int64); wt = (2 * np.arange(16) + 1)[None, :, None]
    for t in range(RO):
        for q in range(N):
            v = np.take_along_axis(x[q], b[q].reshape(8, 1, 16 * I), 2).reshape(8, 16, 16, I)
            gq = g[q][:, :, None, :]
            over = np.sum(v > gq + GAP, axis=1); under = np.sum(v <= gq, axis=1)
            dead = over >= DR + (deaths[q] & 1); imp = ~dead & (under >= IR); und = ~dead & ~imp
            some = np.any(und, axis=1); s = np.argmax(und, axis=1)
            z = np.where(dead, np.take_along_axis(a[q], s[:, None, :], 1), a[q])
            new = np.take_along_axis(tab[q], z, 2)
            vs = np.take_along_axis(v, s[:, None, None, :], 2)[:, :, 0]
            g[q] = np.where(some[:, None, :], np.maximum(g[q], vs), g[q])
            a[q] = np.where(und, a[q], new & (W - 1)); b[q] = np.where(und, b[q], new >> SH)
            deaths[q] = np.sum(dead)
        sent = np.array(g)
        for q in range(N):
            h = sent[(q - 1 - t % (N - 1)) % N]
            if t < RO - 1:
                place = B * np.arange(I) + (np.sum(wt * h, axis=1) & (B - 1))
                place = np.repeat(place[:, None, :], 16, axis=1)
                np.put_along_axis(x[q], place, (np.take_along_axis(x[q], place, 2) + h) >> 1, 2)
            g[q] = np.minimum(sent[q], h + 2)
    return {"yn": a.reshape(N, 128, I).astype(np.float32), "yg": b.reshape(N, 128, I).astype(np.float32), "yl": g.reshape(N, 128, I).astype(np.float32).astype(BF)}

@@ -1,0 +1,457 @@
+from concourse.mybir import dt, AluOpType, AxisListType, ActivationFunctionType
+
+A = AluOpType
+F = ActivationFunctionType
+RO, NS, WX, SH = 4, 256, 4096, 12
+CH = [64, 64, 64, 32, 32]
+OVER_ON_S = (0,)
+RCH = [64, 64, 64, 64]
+R0_ON_V = (2, 3)
+NX = 4
+NM = 4
+
+SCRATCH = {
+    "Xin": ("sbuf", [128, WX], "bfloat16"),
+    "Xw": ("sbuf", [128, WX + 16], "bfloat16"),
+    "Mw": ("sbuf", [128, 4096], "int32"),
+    "RG": ("sbuf", [128, 4096], "float32"),
+    "Gx": ("sbuf", [128, 4096], "bfloat16"),
+    "dd": ("sbuf", [128, 4096], "bfloat16"),
+    "oi": ("sbuf", [128, 4096], "bfloat16"),
+    "ui": ("sbuf", [128, 4096], "bfloat16"),
+    "LA": ("sbuf", [128, 2048], "bfloat16"),
+    "LA2": ("sbuf", [128, 2048], "bfloat16"),
+    "QW": ("sbuf", [128, 2048], "bfloat16"),
+    "EK": ("sbuf", [128, 2048], "float32"),
+    "onesb": ("sbuf", [128, 256], "bfloat16"),
+    "zerob": ("sbuf", [128, 128], "bfloat16"),
+    "onesF": ("sbuf", [128, 128], "float32"),
+    "half": ("sbuf", [128, 256], "bfloat16"),
+    "BO": ("sbuf", [128, 128], "bfloat16"),
+    "BOh": ("sbuf", [128, 128], "bfloat16"),
+    "TL": ("sbuf", [128, 128], "bfloat16"),
+    "TLh": ("sbuf", [128, 128], "bfloat16"),
+    "SB": ("sbuf", [128, 128], "bfloat16"),
+    "TP": ("sbuf", [128, 128], "bfloat16"),
+    "TPh": ("sbuf", [128, 128], "bfloat16"),
+    "EQ": ("sbuf", [128, 128], "float32"),
+    "I1": ("sbuf", [128, 128], "bfloat16"),
+    "IN1": ("sbuf", [128, 128], "bfloat16"),
+    "IP": ("sbuf", [128, 128], "bfloat16"),
+    "IN4": ("sbuf", [128, 128], "bfloat16"),
+    "CP": ("sbuf", [128, 128], "bfloat16"),
+    "CN": ("sbuf", [128, 128], "bfloat16"),
+    "pi": ("sbuf", [128, 1], "int32"),
+    "pa": ("sbuf", [128, 1], "int32"),
+    "pmf": ("sbuf", [128, 1], "float32"),
+    "kk": ("sbuf", [128, 16], "float32"),
+    "rm": ("sbuf", [128, 16], "float32"),
+    "wt": ("sbuf", [128, 1], "float32"),
+    "Ck": ("sbuf", [128, 1], "float32"),
+    "zz": ("sbuf", [128, 1], "float32"),
+    "thr": ("sbuf", [128, 1], "float32"),
+    "c256": ("sbuf", [128, 16], "int32"),
+    "p16": ("sbuf", [128, 16], "int32"),
+    "p16a": ("sbuf", [128, 16], "int32"),
+    "base": ("sbuf", [128, 16], "int32"),
+    "nin": ("sbuf", [128, 256], "int32"),
+    "gin": ("sbuf", [128, 256], "int32"),
+    "lin": ("sbuf", [128, 256], "bfloat16"),
+    "UK": ("sbuf", [128, 1024], "uint16"),
+    "UL": ("sbuf", [128, 1024], "uint16"),
+    "KF": ("sbuf", [128, 1024], "float16"),
+    "LF": ("sbuf", [128, 1024], "float16"),
+    "Wi": ("sbuf", [128, 1280], "int32"),
+    "w0": ("sbuf", [128, 256], "int32"),
+    "G": ("sbuf", [128, 1280], "bfloat16"),
+    "G4": ("sbuf", [128, 1024], "bfloat16"),
+    "H": ("sbuf", [128, 1024], "bfloat16"),
+    "H2": ("sbuf", [128, 1024], "bfloat16"),
+    "Hp": ("sbuf", [128, 1024], "float32"),
+    "dead": ("sbuf", [128, 1024], "bfloat16"),
+    "sgn": ("sbuf", [128, 1024], "bfloat16"),
+    "imp": ("sbuf", [128, 1024], "bfloat16"),
+    "junk": ("sbuf", [128, 1024], "bfloat16"),
+    "acc": ("sbuf", [128, 4], "float32"),
+    "Tt": ("sbuf", [128, 4], "float32"),
+    "ti": ("sbuf", [128, 4], "int32"),
+    "tj": ("sbuf", [128, 4], "int32"),
+    "AK": ("sbuf", [128, 1024], "float16"),
+    "AL": ("sbuf", [128, 1024], "float16"),
+    "kl": ("sbuf", [128, 64], "uint16"),
+    "ll": ("sbuf", [128, 64], "uint16"),
+    "ql": ("sbuf", [128, 64], "uint16"),
+    "q1": ("sbuf", [128, 64], "int32"),
+    "q2": ("sbuf", [128, 64], "int32"),
+    "q3": ("sbuf", [128, 64], "int32"),
+    "yb": ("sbuf", [128, 256], "bfloat16"),
+    "t1": ("sbuf", [128, 256], "float32"),
+    "g1": ("sbuf", [128, 256], "float32"),
+    "t2": ("sbuf", [128, 256], "float32"),
+    "L32": ("sbuf", [128, 256], "int32"),
+    "K32": ("sbuf", [128, 256], "int32"),
+    "ynf": ("sbuf", [128, 256], "float32"),
+    "ygf": ("sbuf", [128, 256], "float32"),
+    "ylb": ("sbuf", [128, 256], "bfloat16"),
+    "gsh": ("sbuf", [128, 256], "bfloat16"),
+    "pO": ("psum", [128, 512], "float32"),
+    "pU": ("psum", [128, 512], "float32"),
+    "pK": ("psum", [128, 512], "float32"),
+    "pL": ("psum", [128, 512], "float32"),
+    "pF": ("psum", [128, 512], "float32"),
+    "pA": ("psum", [128, 512], "float32"),
+    "pB": ("psum", [128, 512], "float32"),
+    "pR": ("psum", [128, 512], "float32"),
+}
+SEMAPHORES = (["cv", "cs", "ct", "cg", "dn", "dg", "dl", "on", "og", "ol"] + ["dx%d" % j for j in range(NX)]
+              + ["dm%d" % j for j in range(NM)] + ["arr%d" % t for t in range(RO)] + ["loc%d" % t for t in range(RO)])
+
+
+def rank_program(g, core, T, topo):
+    rank = T.rank_of(core)
+    if rank is None:
+        return
+    n_ranks = len(T.cores)
+    queue = {"v": g.vector, "s": g.scalar, "t": g.tensor, "g": g, "y": g.sync}
+    count = {"v": 0, "s": 0, "t": 0, "g": 0}
+    clock = {q: {} for q in queue}
+    snap = {}
+    last_w, readers, bank_acc, total = {}, {}, {}, {}
+
+    def meet(q, needs):
+        for s in sorted(needs):
+            v = needs[s]
+            if clock[q].get(s, 0) >= v:
+                continue
+            queue[q].wait_ge(T.sem[s], v)
+            for s2, v2 in snap.get((s, v), {}).items():
+                if clock[q].get(s2, 0) < v2:
+                    clock[q][s2] = v2
+            clock[q][s] = v
+
+    def deps(q, reads, writes, banks):
+        own = "c" + q
+        needs = {}
+
+        def add(ev):
+            if ev[1] > needs.get(ev[0], 0):
+                needs[ev[0]] = ev[1]
+        for r in reads:
+            if r in last_w:
+                add(last_w[r])
+        for w in writes:
+            if w in last_w and not (q == "t" and last_w[w][0] == own):
+                add(last_w[w])
+            for s, v in readers.get(w, {}).items():
+                if s != own:
+                    add((s, v))
+        for b in banks:
+            for s, v in bank_acc.get(b, {}).items():
+                if s != own:
+                    add((s, v))
+        return needs
+
+    def record(ev, reads, writes, banks):
+        for r in reads:
+            d = readers.setdefault(r, {})
+            d[ev[0]] = max(d.get(ev[0], 0), ev[1])
+        for w in writes:
+            last_w[w] = ev
+            readers[w] = {}
+        for b in banks:
+            bank_acc.setdefault(b, {})[ev[0]] = ev[1]
+
+    def op(q, fn, reads=(), writes=(), banks=()):
+        meet(q, deps(q, reads, writes, banks))
+        ins = fn()
+        count[q] += 1
+        ev = ("c" + q, count[q])
+        ins.then_inc(T.sem[ev[0]], 1)
+        total[ev[0]] = count[q]
+        snap[ev] = dict(clock[q])
+        record(ev, reads, writes, banks)
+
+    def dma(q, sem, out, in_, reads=(), writes=()):
+        meet(q, deps(q, reads, writes, ()))
+        queue[q].dma_start(out, in_).then_inc(T.sem[sem], 16)
+        ev = (sem, 16)
+        total[sem] = 16
+        snap[ev] = dict(clock[q])
+        record(ev, reads, writes, ())
+
+    V, S, P = g.vector, g.scalar, g.tensor
+
+    xs = WX // NX
+    ms = 4096 // NM
+    dma("y", "dg", T.gin[:], T.grd[:], writes=["gin"])
+    dma("s", "dl", T.lin[:], T.lim[:], writes=["lin"])
+    dma("s", "dn", T.nin[:], T.nam[:], writes=["nin"])
+    for j in range(NX):
+        dma("y" if j % 2 == 0 else "s", "dx%d" % j, T.Xin[:, j * xs:(j + 1) * xs], T.xc[:, j * xs:(j + 1) * xs], writes=["xin%d" % j])
+    for j in range(NM):
+        dma("y", "dm%d" % j, T.Mw[:, j * ms:(j + 1) * ms], T.rel[:, j * ms:(j + 1) * ms], writes=["mw%d" % j])
+    MW = ["mw%d" % j for j in range(NM)]
+
+    def ms_(name, val, cols=None):
+        op("v", lambda: V.memset(T[name][:] if cols is None else T[name][:, cols[0]:cols[1]], val), writes=[name])
+    ms_("onesb", 1.0)
+    ms_("onesF", 1.0)
+    ms_("zerob", 0.0)
+    op("g", lambda: g.iota(T.pi[:], [[0, 1]], 0, 1), writes=["pi"])
+    op("g", lambda: g.affine_select(T.BO[:], T.onesb[:, 0:128], [[-16, 8], [0, 16]], A.is_ge, 0.0, 0, 1), ["onesb"], ["BO"])
+    op("g", lambda: g.affine_select(T.BO[:], T.BO[:], [[16, 8], [0, 16]], A.is_ge, 0.0, 15, -1), ["BO"], ["BO"])
+    op("g", lambda: g.iota(T.kk[:], [[1, 16]], 0, 0, allow_small_or_imprecise_dtypes=True), writes=["kk"])
+    op("g", lambda: g.affine_select(T.EQ[:], T.onesF[:], [[-1, 128]], A.is_equal, 0.0, 0, 1), ["onesF"], ["EQ"])
+    op("g", lambda: g.affine_select(T.SB[:], T.BO[:], [[1, 128]], A.is_gt, 0.0, 0, -1), ["BO"], ["SB"])
+    op("g", lambda: g.affine_select(T.SB[:], T.SB[:], [[1, 128]], A.not_equal, -1.0, 0, -1), ["SB"], ["SB"])
+    op("g", lambda: g.affine_select(T.TL[:], T.SB[:], [[0, 128]], A.is_equal, 0.0, 0, 0), ["SB"], ["TL"])
+    op("g", lambda: g.affine_select(T.TL[:, 0:128:16], T.BO[:, 0:128:16], [[16, 8]], A.not_equal, -17.0, 0, -1), ["BO", "TL"], ["TL"])
+    for nm, sg in (("CP", 1.0), ("CN", -1.0)):
+        op("g", lambda nm=nm, sg=sg: g.affine_select(T[nm][:], T.zerob[:], [[0, 128]], A.not_equal, sg * 8388608.0, 0, 1), ["zerob"], [nm])
+        op("g", lambda nm=nm, sg=sg: g.affine_select(T[nm][:], T[nm][:], [[0, 128]], A.not_equal, sg * 2048.0, -1, 1), [nm], [nm])
+    op("g", lambda: g.iota(T.c256[:], [[256, 16]], 0, 0), writes=["c256"])
+    op("g", lambda: g.iota(T.p16[:], [[0, 16]], 0, 16), writes=["p16"])
+
+    ms_("LA", 0.0)
+    op("v", lambda: V.memset(T.Xw[:, 0:16], 0.0), writes=["X0"])
+    op("v", lambda: V.memset(T.Tt[:, 0:1], 5.5), writes=["Tt0"])
+    op("v", lambda: V.tensor_scalar(T.pa[:], T.pi[:], 15, None, A.bitwise_and), ["pi"], ["pa"])
+    op("v", lambda: V.tensor_copy(T.pmf[:], T.pa[:]), ["pa"], ["pmf"])
+    op("v", lambda: V.tensor_scalar(T.rm[:], T.kk[:], T.pmf[:, 0:1], None, A.is_equal), ["kk", "pmf"], ["rm"])
+    op("v", lambda: V.tensor_scalar(T.wt[:], T.pmf[:], 2.0, 1.0, A.mult, A.add), ["pmf"], ["wt"])
+    for a in range(16):
+        op("v", lambda a=a: V.tensor_copy(T.LA[:, a * 129:(a + 1) * 128:16], T.BO[:, 0:128:16]), ["BO", "LA"] if a == 0 else ["BO"], ["LAk%d" % a])
+    LA = ["LAk%d" % a for a in range(16)]
+
+    for nm, src, sc in (("TP", "SB", 8192.0), ("TPh", "SB", 4096.0), ("TLh", "TL", 0.5), ("BOh", "BO", 0.5), ("I1", "EQ", 1.0),
+                        ("IN1", "EQ", -1.0), ("IP", "EQ", 4096.0), ("IN4", "EQ", -4096.0)):
+        op("s", lambda nm=nm, src=src, sc=sc: S.activation(T[nm][:], T[src][:], F.Copy, scale=sc), [src], [nm])
+    op("s", lambda: S.activation(T.LA2[:], T.LA[:], F.Copy, scale=0.5), LA, ["LA2"])
+    for k in range(16):
+        op("s", lambda k=k: S.activation(T.EK[:, k * 128:(k + 1) * 128], T.EQ[:], F.Copy, scale=T.rm[:, k:k + 1]), ["EQ", "rm"], ["EK%d" % k])
+    op("s", lambda: S.activation(T.QW[:], T.LA[:], F.Copy, scale=T.wt[:, 0:1]), LA + ["wt"], ["QW"])
+
+    def sl(name, t, w=NS):
+        return T[name][:, t * w:(t + 1) * w]
+
+    XWIN = T.Xw[:, 16:WX + 16]
+
+    def expand(k, t):
+        op("v", lambda: V.tensor_copy(T.Gx[:, k:4096:16], sl("G", t)), ["G%d" % t], ["Gx%d" % k])
+    GX = ["Gx%d" % k for k in range(16)]
+
+    op("v", lambda: V.tensor_scalar(sl("G", 0), T.lin[:], 128.0, None, A.add), ["lin"], ["G0"])
+    for k in range(16):
+        expand(k, 0)
+    op("v", lambda: V.tensor_copy(sl("UK", 0), T.gin[:]), ["gin"], ["UK0"])
+    op("v", lambda: V.tensor_copy(sl("UL", 0), T.nin[:]), ["nin"], ["UL0"])
+    op("v", lambda: V.tensor_scalar(sl("KF", 0), T.gin[:], -2048.0, None, A.add), ["gin"], ["KF0"])
+    op("v", lambda: V.tensor_scalar(sl("LF", 0), T.nin[:], -2048.0, None, A.add), ["nin"], ["LF0"])
+    op("v", lambda: V.tensor_scalar(T.w0[:], T.gin[:], 4096.0, None, A.mult), ["gin"], ["w0"])
+    op("v", lambda: V.tensor_scalar(T.Ck[:], T.pmf[:], -4096.0, -4096.0, A.mult, A.add), ["pmf"], ["Ck"])
+    op("v", lambda: V.tensor_scalar(T.zz[:], T.pmf[:], 0.0, -1.5, A.is_equal, A.mult), ["pmf"], ["zz"])
+    op("v", lambda: V.tensor_tensor(sl("Wi", 0), T.w0[:], T.nin[:], A.add), ["w0", "nin"], ["Wi0"])
+    op("v", lambda: V.tensor_scalar(T.thr[:], T.pmf[:], 0.5, T.zz[:, 0:1], A.mult, A.add), ["pmf", "zz"], ["thr"])
+    for j in range(NX):
+        op("v", lambda j=j: V.tensor_scalar(T.Xw[:, 16 + j * xs:16 + (j + 1) * xs], T.Xin[:, j * xs:(j + 1) * xs], 128.0, None, A.add),
+           ["xin%d" % j], ["X%d" % (j + 1)])
+    X = ["X%d" % j for j in range(NX + 1)]
+
+    def release_chunk(t, c, q):
+        n = RCH[c]
+        c0 = sum(RCH[:c])
+        off = T.UL[:, t * NS + c0:t * NS + c0 + n]
+        dst = T.RG[:, 16 * c0:16 * (c0 + n)]
+        if q == "v":
+            op("v", lambda: V.tensor_copy(dst, T.Mw[:, 0:4096].indirect(off)), MW + ["UL%d" % t], ["RG%d" % c])
+        else:
+            op("s", lambda: S.activation(dst, T.Mw[:, 0:4096].indirect(off), F.Copy), MW + ["UL%d" % t], ["RG%d" % c])
+
+    def release_pick(t, c):
+        n = RCH[c]
+        c0 = sum(RCH[:c])
+        o = T.pR[:, c0:c0 + n]
+        w = ["pR%d" % c]
+        op("t", lambda: P.matmul(o, T.IN4[:], T.KF[:, t * NS + c0:t * NS + c0 + n], True, False), ["IN4", "KF%d" % t], w, ["pR"])
+        op("t", lambda: P.matmul(o, T.IN1[:], T.LF[:, t * NS + c0:t * NS + c0 + n], False, False), ["IN1", "LF%d" % t], w, ["pR"])
+        op("t", lambda: P.matmul(o, T.CN[:], T.onesb[:, 0:n], False, False), ["CN", "onesb"], w, ["pR"])
+        for k in range(16):
+            op("t", lambda k=k: P.matmul(o, T.EK[:, k * 128:(k + 1) * 128], T.RG[:, 16 * c0 + k:16 * (c0 + n):16], False, k == 15),
+               ["EK%d" % k, "RG%d" % c], w, ["pR"])
+
+    nch = len(CH)
+    starts = [sum(CH[:c]) for c in range(nch)]
+
+    for t in range(RO):
+        G, G4, H = sl("G", t), sl("G4", t), sl("H", t)
+        last = t == RO - 1
+
+        def gather(c):
+            a, b = starts[c], starts[c] + CH[c]
+            op("v", lambda: V.tensor_tensor(T.dd[:, 16 * a:16 * b], XWIN.indirect(T.UK[:, t * NS + a:t * NS + b]), T.Gx[:, 16 * a:16 * b], A.subtract),
+               X + GX + ["UK%d" % t], ["dd%d" % c])
+
+        def under(c):
+            a, b = starts[c], starts[c] + CH[c]
+            op("s", lambda: S.activation(T.ui[:, 16 * a:16 * b], T.dd[:, 16 * a:16 * b], F.Sign, bias=0.5, scale=-1.0),
+               ["dd%d" % c], ["ui%d" % c])
+
+        def over(c):
+            a, b = starts[c], starts[c] + CH[c]
+            if c in OVER_ON_S:
+                op("s", lambda: S.activation(T.oi[:, 16 * a:16 * b], T.dd[:, 16 * a:16 * b], F.Sign, bias=-4.5, scale=1.0), ["dd%d" % c], ["oi%d" % c])
+            else:
+                op("v", lambda: V.tensor_scalar(T.oi[:, 16 * a:16 * b], T.dd[:, 16 * a:16 * b], 4.0, None, A.is_gt), ["dd%d" % c], ["oi%d" % c])
+
+        def counts(c):
+            a, n = starts[c], CH[c]
+            oo, uu = T.pO[:, a:a + n], T.pU[:, a:a + n]
+            m, mk = ("LA2", lambda k: "LA2") if c in OVER_ON_S else ("LA", lambda k: "LAk%d" % k)
+
+            def overs():
+                if c in OVER_ON_S:
+                    op("t", lambda: P.matmul(oo, T.BOh[:], T.onesb[:, 0:n], True, False), ["BOh", "onesb"], ["pO%d" % c], ["pO"])
+                for k in range(16):
+                    op("t", lambda k=k: P.matmul(oo, T[m][:, k * 128:(k + 1) * 128], T.oi[:, 16 * a + k:16 * (a + n):16], k == 0 and c not in OVER_ON_S, k == 15),
+                       [mk(k), "oi%d" % c], ["pO%d" % c], ["pO"])
+
+            def unders():
+                for k in range(16):
+                    op("t", lambda k=k: P.matmul(uu, T.LA[:, k * 128:(k + 1) * 128], T.ui[:, 16 * a + k:16 * (a + n):16], k == 0, k == 15),
+                       ["LAk%d" % k, "ui%d" % c], ["pU%d" % c], ["pU"])
+            if c in OVER_ON_S:
+                unders()
+                overs()
+            else:
+                overs()
+                unders()
+
+        if t > 0:
+            for c in range(len(RCH)):
+                release_pick(t, c)
+        gather(0)
+        for c in range(nch):
+            if c + 1 < nch:
+                gather(c + 1)
+            under(c)
+            over(c)
+            if c == nch - 1:
+                op("t", lambda: P.matmul(T.pK[:, 0:NS], T.I1[:], sl("KF", t), True, False), ["I1", "KF%d" % t], ["pKa"], ["pK"])
+            counts(c)
+
+        OC, UC = ["pO%d" % c for c in range(nch)], ["pU%d" % c for c in range(nch)]
+        dead, sgn, imp = sl("dead", t), sl("sgn", t), sl("imp", t)
+        op("v", lambda: V.tensor_scalar(dead, T.pO[:, 0:NS], T.Tt[:, t:t + 1], None, A.is_gt), OC + ["Tt%d" % t], ["dead"], ["pO"])
+        op("s", lambda: S.activation(sgn, T.pU[:, 0:NS], F.Sign, bias=-7.0), UC, ["sgn"], ["pU"])
+        op("t", lambda: P.matmul(T.pK[:, 0:NS], T.TP[:], dead, False, False), ["TP", "dead"], ["pKa"], ["pK"])
+        op("t", lambda: P.matmul(T.pK[:, 0:NS], T.TPh[:], sgn, False, True), ["TPh", "sgn"], ["pKa"], ["pK"])
+        op("t", lambda: P.matmul(T.pL[:, 0:NS], T.TL[:], dead, True, False), ["TL", "dead"], ["pL"], ["pL"])
+        op("t", lambda: P.matmul(T.pL[:, 0:NS], T.TLh[:], sgn, False, True), ["TLh", "sgn"], ["pL"], ["pL"])
+        AK, AL = sl("AK", t), sl("AL", t)
+        op("v", lambda: V.tensor_scalar(AK, T.pK[:, 0:NS], T.Ck[:, 0:1], -2064.0, A.add, A.max), ["pKa", "Ck"], ["AK"], ["pK"])
+        for a in range(16):
+            op("t", lambda a=a: P.matmul(T.pA[:, 0:16], T.LA[:, a * 128:(a + 1) * 128], T.AK[:, t * NS + a:(t + 1) * NS:16], a == 0, a == 15),
+               ["LAk%d" % a, "AK"], ["pA0"], ["pA"])
+        op("v", lambda: V.tensor_scalar(T.pF[:, 0:NS], T.pL[:, 0:NS], T.thr[:, 0:1], None, A.is_ge), ["pL", "thr"], ["pF"], ["pL", "pF"])
+        op("v", lambda: V.tensor_tensor(AL, T.pF[:, 0:NS], sl("LF", t), A.mult), ["pF", "LF%d" % t], ["AL"], ["pF"])
+        op("s", lambda: S.activation(imp, sgn, F.Relu), ["sgn"], ["imp"])
+        if not last:
+            op("s", lambda: S.activation(sl("junk", t), dead, F.Copy, accum_out=T.acc[:, t:t + 1]), ["dead"], ["junk", "acc"])
+
+        kl, ll, ql = sl("kl", t, 16), sl("ll", t, 16), sl("ql", t, 16)
+        op("v", lambda: V.tensor_scalar(kl, T.pA[:, 0:16], 33024.0, None, A.add), ["pA0"], ["kl"], ["pA"])
+        op("v", lambda: V.tensor_tensor(G4, T.Xw[:, 0:WX + 16].indirect(kl), G, A.max), X + ["kl", "G%d" % t], ["G4%d" % t])
+        dst = T.cores[(rank + 1 + t % (n_ranks - 1)) % n_ranks]
+        rid, pid, _ = topo.addr(dst)
+        eng = topo.engines(core, dst)[::2]
+        meet("g", deps("g", ["G4%d" % t], [], ()))
+        g.remote_dma(H, G4, T.sem["arr%d" % t], T.sem["loc%d" % t], pid, rid, sum(1 << e for e in eng))
+        total["arr%d" % t] = len(eng)
+        total["loc%d" % t] = len(eng)
+        last_w["H%d" % t] = ("arr%d" % t, len(eng))
+
+        for a in range(16):
+            op("t", lambda a=a: P.matmul(T.pB[:, 0:16], T.LA[:, a * 128:(a + 1) * 128], T.AL[:, t * NS + a:(t + 1) * NS:16], a == 0, a == 15),
+               ["LAk%d" % a, "AL"], ["pB"], ["pB"])
+        op("v", lambda: V.tensor_scalar(ll, T.pB[:, 0:16], 2048.0, None, A.add), ["pB"], ["ll"], ["pB"])
+        op("v", lambda: V.tensor_tensor(T.g1[:], T.Mw[:, 0:4096].indirect(ll), sl("Wi", t), A.subtract), MW + ["ll", "Wi%d" % t], ["g1"])
+        if t == 0:
+            sc = [c for c in range(len(RCH)) if c not in R0_ON_V]
+            for c in range(max(len(sc), len(R0_ON_V))):
+                for lst, q in ((sc, "s"), (R0_ON_V, "v")):
+                    if c < len(lst):
+                        release_chunk(0, lst[c], q)
+            for c in range(max(len(sc), len(R0_ON_V))):
+                for lst in (sc, R0_ON_V):
+                    if c < len(lst):
+                        release_pick(0, lst[c])
+        op("v", lambda: V.tensor_tensor(T.t2[:], T.g1[:], dead, A.mult), ["g1", "dead"], ["t2"])
+        W1 = T.pK[:, NS:2 * NS]
+        op("v", lambda: V.tensor_tensor(T.t1[:], T.pR[:, 0:NS], imp, A.mult), ["pR%d" % c for c in range(len(RCH))] + ["imp"], ["t1"], ["pR"])
+        op("t", lambda: P.matmul(W1, T.IP[:], sl("KF", t), True, False), ["IP", "KF%d" % t], ["pKb"], ["pK"])
+        op("t", lambda: P.matmul(W1, T.I1[:], sl("LF", t), False, False), ["I1", "LF%d" % t], ["pKb"], ["pK"])
+        op("t", lambda: P.matmul(W1, T.CP[:], T.onesb[:], False, False), ["CP", "onesb"], ["pKb"], ["pK"])
+        op("t", lambda: P.matmul(W1, T.EQ[:], T.t1[:], False, True), ["EQ", "t1"], ["pKb"], ["pK"])
+        if not last:
+            op("t", lambda: P.matmul(T.pB[:, 32:33], T.onesF[:], T.acc[:, t:t + 1], True, True), ["onesF", "acc"], ["pBp"], ["pB"])
+            op("v", lambda: V.tensor_copy(T.ti[:, t:t + 1], T.pB[:, 32:33]), ["pBp"], ["ti"], ["pB"])
+            op("v", lambda: V.tensor_scalar(T.tj[:, t:t + 1], T.ti[:, t:t + 1], 1, None, A.bitwise_and), ["ti"], ["tj"])
+        Wn = sl("Wi", t + 1)
+        op("v", lambda: V.tensor_tensor(Wn, W1, T.t2[:], A.add), ["pKb", "t2"], ["Wi%d" % (t + 1)], ["pK"])
+        if not last:
+            op("v", lambda: V.tensor_scalar(T.Tt[:, t + 1:t + 2], T.tj[:, t:t + 1], 5.5, None, A.add), ["tj"], ["Tt%d" % (t + 1)])
+        op("v", lambda: V.tensor_scalar(T.L32[:], Wn, 4095, None, A.bitwise_and), ["Wi%d" % (t + 1)], ["L32"])
+        op("v", lambda: V.tensor_scalar(T.K32[:], Wn, SH, None, A.logical_shift_right), ["Wi%d" % (t + 1)], ["K32"])
+
+        if last:
+            op("v", lambda: V.tensor_copy(T.ynf[:], T.L32[:]), ["L32"], ["ynf"])
+            dma("y", "on", T.yn[:], T.ynf[:], ["ynf"])
+            op("v", lambda: V.tensor_copy(T.ygf[:], T.K32[:]), ["K32"], ["ygf"])
+            dma("s", "og", T.yg[:], T.ygf[:], ["ygf"])
+            op("v", lambda: V.tensor_scalar(T.gsh[:], G4, -128.0, None, A.add), ["G4%d" % t], ["gsh"])
+            op("v", lambda: V.tensor_scalar(sl("H2", t), H, -126.0, None, A.add), ["H%d" % t], ["H2"])
+            op("v", lambda: V.tensor_tensor(T.ylb[:], T.gsh[:], sl("H2", t), A.min), ["gsh", "H2"], ["ylb"])
+            dma("y", "ol", T.yl[:], T.ylb[:], ["ylb"])
+            break
+
+        op("v", lambda: V.tensor_copy(sl("UL", t + 1), T.L32[:]), ["L32"], ["UL%d" % (t + 1)])
+        for c in range(len(RCH)):
+            release_chunk(t + 1, c, "s")
+
+        fill = [lambda: op("v", lambda: V.tensor_copy(sl("UK", t + 1), T.K32[:]), ["K32"], ["UK%d" % (t + 1)]),
+                lambda: op("v", lambda: V.tensor_scalar(sl("LF", t + 1), T.L32[:], -2048.0, None, A.add), ["L32"], ["LF%d" % (t + 1)]),
+                lambda: op("v", lambda: V.tensor_scalar(sl("KF", t + 1), T.K32[:], -2048.0, None, A.add), ["K32"], ["KF%d" % (t + 1)])]
+        for k in range(16):
+            fill.append(lambda k=k: expand(k, t + 1))
+
+        def filler(n):
+            for _ in range(n):
+                if fill:
+                    fill.pop(0)()
+        if t == 0:
+            op("v", lambda: V.tensor_scalar(T.p16a[:], T.p16[:], 255, None, A.bitwise_and), ["p16"], ["p16a"])
+            op("v", lambda: V.memset(T.half[:], 0.5), writes=["half"])
+            op("v", lambda: V.tensor_tensor(T.base[:], T.p16a[:], T.c256[:], A.add), ["p16a", "c256"], ["base"])
+        for a in range(16):
+            op("t", lambda a=a: P.matmul(T.pA[:, 16:32], T.QW[:, a * 128:(a + 1) * 128], T.H[:, t * NS + a:(t + 1) * NS:16], a == 0, a == 15),
+               ["QW", "H%d" % t], ["pA1"], ["pA"])
+        q1, q2, q3 = sl("q1", t, 16), sl("q2", t, 16), sl("q3", t, 16)
+        filler(2)
+        op("v", lambda: V.tensor_scalar(sl("H2", t), H, 2.0, None, A.add), ["H%d" % t], ["H2"])
+        op("v", lambda: V.tensor_scalar(sl("Hp", t), H, -0.25, None, A.add), ["H%d" % t], ["Hp"])
+        op("v", lambda: V.tensor_tensor(sl("G", t + 1), G4, sl("H2", t), A.min), ["G4%d" % t, "H2"], ["G%d" % (t + 1)])
+        op("v", lambda: V.tensor_copy(q1, T.pA[:, 16:32]), ["pA1"], ["q1"], ["pA"])
+        filler(1)
+        op("v", lambda: V.tensor_scalar(q2, q1, 15, None, A.bitwise_and), ["q1"], ["q2"])
+        filler(1)
+        op("v", lambda: V.tensor_tensor(q3, q2, T.base[:], A.add), ["q2", "base"], ["q3"])
+        filler(1)
+        op("v", lambda: V.tensor_copy(ql, q3), ["q3"], ["ql"])
+        filler(1)
+        op("v", lambda: V.tensor_tensor(T.yb[:], XWIN.indirect(ql), sl("Hp", t), A.add), X + ["ql", "Hp"], ["yb"])
+        filler(2)
+        op("v", lambda: V.tensor_tensor(XWIN.indirect(ql), T.yb[:], T.half[:], A.mult), ["yb", "half", "ql"], X)
+        filler(99)
+
+    for s in sorted(total):
+        meet("g", {s: total[s]})

@@ -3,24 +3,32 @@ from concourse.mybir import dt, AluOpType, AxisListType, ActivationFunctionType
 A = AluOpType
 F = ActivationFunctionType
 RO, NS, WX, SH = 4, 256, 4096, 12
-CH = [64, 64, 64, 32, 32]
-OVER_ON_S = (0,)
+CH = [64, 64, 64, 64]
+OVER_ON_S = (1,)
 RCH = [64, 64, 64, 64]
-R0_ON_V = (2, 3)
 NX = 4
 NM = 4
+S0 = {-1: [], 0: [], 1: [], 2: [], 3: []}
+S0_END = ["r0", "r1", "r2"]
+V0_END = ["r3"]
+V0_LATE = ["b0", "b1", "b2", "b3"]
+SHIFT0 = ()
+SHIFT = (2, 3)
+P1 = {0: [0, 1], 1: [], 2: [], 3: []}
+GX_ON_G = (13, 14, 15)
 
 SCRATCH = {
-    "Xin": ("sbuf", [128, WX], "bfloat16"),
+    "Xin": ("sbuf", [128, WX + 16], "bfloat16"),
     "Xw": ("sbuf", [128, WX + 16], "bfloat16"),
     "Mw": ("sbuf", [128, 4096], "int32"),
     "RG": ("sbuf", [128, 4096], "float32"),
+    "RS": ("sbuf", [128, 4096], "float32"),
+    "EQf": ("sbuf", [128, 128], "float32"),
     "Gx": ("sbuf", [128, 4096], "bfloat16"),
     "dd": ("sbuf", [128, 4096], "bfloat16"),
     "oi": ("sbuf", [128, 4096], "bfloat16"),
     "ui": ("sbuf", [128, 4096], "bfloat16"),
     "LA": ("sbuf", [128, 2048], "bfloat16"),
-    "LA2": ("sbuf", [128, 2048], "bfloat16"),
     "QW": ("sbuf", [128, 2048], "bfloat16"),
     "EK": ("sbuf", [128, 2048], "float32"),
     "onesb": ("sbuf", [128, 256], "bfloat16"),
@@ -28,24 +36,23 @@ SCRATCH = {
     "onesF": ("sbuf", [128, 128], "float32"),
     "half": ("sbuf", [128, 256], "bfloat16"),
     "BO": ("sbuf", [128, 128], "bfloat16"),
-    "BOh": ("sbuf", [128, 128], "bfloat16"),
     "TL": ("sbuf", [128, 128], "bfloat16"),
     "TLh": ("sbuf", [128, 128], "bfloat16"),
     "SB": ("sbuf", [128, 128], "bfloat16"),
     "TP": ("sbuf", [128, 128], "bfloat16"),
     "TPh": ("sbuf", [128, 128], "bfloat16"),
-    "EQ": ("sbuf", [128, 128], "float32"),
-    "I1": ("sbuf", [128, 128], "bfloat16"),
-    "IN1": ("sbuf", [128, 128], "bfloat16"),
+    "EQ": ("sbuf", [128, 128], "bfloat16"),
     "IP": ("sbuf", [128, 128], "bfloat16"),
-    "IN4": ("sbuf", [128, 128], "bfloat16"),
+    "IH": ("sbuf", [128, 128], "bfloat16"),
+    "IHn": ("sbuf", [128, 128], "bfloat16"),
+    "IDn": ("sbuf", [128, 128], "bfloat16"),
     "CP": ("sbuf", [128, 128], "bfloat16"),
     "CN": ("sbuf", [128, 128], "bfloat16"),
+    "B2": ("sbuf", [128, 128], "bfloat16"),
+    "B130": ("sbuf", [128, 128], "bfloat16"),
     "pi": ("sbuf", [128, 1], "int32"),
     "pa": ("sbuf", [128, 1], "int32"),
     "pmf": ("sbuf", [128, 1], "float32"),
-    "kk": ("sbuf", [128, 16], "float32"),
-    "rm": ("sbuf", [128, 16], "float32"),
     "wt": ("sbuf", [128, 1], "float32"),
     "Ck": ("sbuf", [128, 1], "float32"),
     "zz": ("sbuf", [128, 1], "float32"),
@@ -61,16 +68,15 @@ SCRATCH = {
     "UL": ("sbuf", [128, 1024], "uint16"),
     "KF": ("sbuf", [128, 1024], "float16"),
     "LF": ("sbuf", [128, 1024], "float16"),
-    "Wi": ("sbuf", [128, 1280], "int32"),
-    "w0": ("sbuf", [128, 256], "int32"),
+    "Wn": ("sbuf", [128, 256], "int32"),
     "G": ("sbuf", [128, 1280], "bfloat16"),
     "G4": ("sbuf", [128, 1024], "bfloat16"),
+    "G4b": ("sbuf", [128, 256], "bfloat16"),
     "H": ("sbuf", [128, 1024], "bfloat16"),
     "H2": ("sbuf", [128, 1024], "bfloat16"),
     "Hp": ("sbuf", [128, 1024], "float32"),
     "dead": ("sbuf", [128, 1024], "bfloat16"),
     "sgn": ("sbuf", [128, 1024], "bfloat16"),
-    "imp": ("sbuf", [128, 1024], "bfloat16"),
     "junk": ("sbuf", [128, 1024], "bfloat16"),
     "acc": ("sbuf", [128, 4], "float32"),
     "Tt": ("sbuf", [128, 4], "float32"),
@@ -85,9 +91,8 @@ SCRATCH = {
     "q2": ("sbuf", [128, 64], "int32"),
     "q3": ("sbuf", [128, 64], "int32"),
     "yb": ("sbuf", [128, 256], "bfloat16"),
-    "t1": ("sbuf", [128, 256], "float32"),
     "g1": ("sbuf", [128, 256], "float32"),
-    "t2": ("sbuf", [128, 256], "float32"),
+    "m1": ("sbuf", [128, 256], "float32"),
     "L32": ("sbuf", [128, 256], "int32"),
     "K32": ("sbuf", [128, 256], "int32"),
     "ynf": ("sbuf", [128, 256], "float32"),
@@ -104,7 +109,7 @@ SCRATCH = {
     "pR": ("psum", [128, 512], "float32"),
 }
 SEMAPHORES = (["cv", "cs", "ct", "cg", "dn", "dg", "dl", "on", "og", "ol"] + ["dx%d" % j for j in range(NX)]
-              + ["dm%d" % j for j in range(NM)] + ["arr%d" % t for t in range(RO)] + ["loc%d" % t for t in range(RO)])
+              + ["dm%d" % j for j in range(NM)] + ["arr%d" % t for t in range(RO)] + ["loc%d" % t for t in range(RO)] + ["rs%d" % j for j in range(RO * len(RCH))])
 
 
 def rank_program(g, core, T, topo):
@@ -183,79 +188,88 @@ def rank_program(g, core, T, topo):
 
     xs = WX // NX
     ms = 4096 // NM
-    dma("y", "dg", T.gin[:], T.grd[:], writes=["gin"])
     dma("s", "dl", T.lin[:], T.lim[:], writes=["lin"])
+    dma("y", "dg", T.gin[:], T.grd[:], writes=["gin"])
     dma("s", "dn", T.nin[:], T.nam[:], writes=["nin"])
     for j in range(NX):
-        dma("y" if j % 2 == 0 else "s", "dx%d" % j, T.Xin[:, j * xs:(j + 1) * xs], T.xc[:, j * xs:(j + 1) * xs], writes=["xin%d" % j])
+        dma("y", "dx%d" % j, T.Xin[:, 16 + j * xs:16 + (j + 1) * xs], T.xc[:, j * xs:(j + 1) * xs], writes=["xin%d" % j])
     for j in range(NM):
         dma("y", "dm%d" % j, T.Mw[:, j * ms:(j + 1) * ms], T.rel[:, j * ms:(j + 1) * ms], writes=["mw%d" % j])
     MW = ["mw%d" % j for j in range(NM)]
 
-    def ms_(name, val, cols=None):
-        op("v", lambda: V.memset(T[name][:] if cols is None else T[name][:, cols[0]:cols[1]], val), writes=[name])
-    ms_("onesb", 1.0)
-    ms_("onesF", 1.0)
-    ms_("zerob", 0.0)
+    def fill(name, val):
+        op("v", lambda: V.memset(T[name][:], val), writes=[name])
+
+    def select(out, in_, pattern, cmp, val, base, mult, reads, writes):
+        op("g", lambda: g.affine_select(out, in_, pattern, cmp, val, base, mult), reads, writes)
+
+    fill("onesb", 1.0)
+    fill("zerob", 0.0)
+    select(T.BO[:], T.onesb[:, 0:128], [[-16, 8], [0, 16]], A.is_ge, 0.0, 0, 1, ["onesb"], ["BO"])
+    select(T.BO[:], T.BO[:], [[16, 8], [0, 16]], A.is_ge, 0.0, 15, -1, ["BO"], ["BO"])
     op("g", lambda: g.iota(T.pi[:], [[0, 1]], 0, 1), writes=["pi"])
-    op("g", lambda: g.affine_select(T.BO[:], T.onesb[:, 0:128], [[-16, 8], [0, 16]], A.is_ge, 0.0, 0, 1), ["onesb"], ["BO"])
-    op("g", lambda: g.affine_select(T.BO[:], T.BO[:], [[16, 8], [0, 16]], A.is_ge, 0.0, 15, -1), ["BO"], ["BO"])
-    op("g", lambda: g.iota(T.kk[:], [[1, 16]], 0, 0, allow_small_or_imprecise_dtypes=True), writes=["kk"])
-    op("g", lambda: g.affine_select(T.EQ[:], T.onesF[:], [[-1, 128]], A.is_equal, 0.0, 0, 1), ["onesF"], ["EQ"])
-    op("g", lambda: g.affine_select(T.SB[:], T.BO[:], [[1, 128]], A.is_gt, 0.0, 0, -1), ["BO"], ["SB"])
-    op("g", lambda: g.affine_select(T.SB[:], T.SB[:], [[1, 128]], A.not_equal, -1.0, 0, -1), ["SB"], ["SB"])
-    op("g", lambda: g.affine_select(T.TL[:], T.SB[:], [[0, 128]], A.is_equal, 0.0, 0, 0), ["SB"], ["TL"])
-    op("g", lambda: g.affine_select(T.TL[:, 0:128:16], T.BO[:, 0:128:16], [[16, 8]], A.not_equal, -17.0, 0, -1), ["BO", "TL"], ["TL"])
-    for nm, sg in (("CP", 1.0), ("CN", -1.0)):
-        op("g", lambda nm=nm, sg=sg: g.affine_select(T[nm][:], T.zerob[:], [[0, 128]], A.not_equal, sg * 8388608.0, 0, 1), ["zerob"], [nm])
-        op("g", lambda nm=nm, sg=sg: g.affine_select(T[nm][:], T[nm][:], [[0, 128]], A.not_equal, sg * 2048.0, -1, 1), [nm], [nm])
     op("g", lambda: g.iota(T.c256[:], [[256, 16]], 0, 0), writes=["c256"])
     op("g", lambda: g.iota(T.p16[:], [[0, 16]], 0, 16), writes=["p16"])
+    select(T.EQ[:], T.onesb[:, 0:128], [[-1, 128]], A.is_equal, 0.0, 0, 1, ["onesb"], ["EQ"])
+    select(T.SB[:], T.BO[:], [[1, 128]], A.is_gt, 0.0, 0, -1, ["BO"], ["SB"])
+    select(T.SB[:], T.SB[:], [[1, 128]], A.not_equal, -1.0, 0, -1, ["SB"], ["SB"])
+    select(T.TL[:], T.SB[:], [[0, 128]], A.is_equal, 0.0, 0, 0, ["SB"], ["TL"])
+    select(T.TL[:, 0:128:16], T.BO[:, 0:128:16], [[16, 8]], A.not_equal, -17.0, 0, -1, ["BO", "TL"], ["TL"])
 
-    ms_("LA", 0.0)
+    fill("LA", 0.0)
+    op("v", lambda: V.memset(T.Xin[:, 0:16], 0.0), writes=["xinz"])
     op("v", lambda: V.memset(T.Xw[:, 0:16], 0.0), writes=["X0"])
-    op("v", lambda: V.memset(T.Tt[:, 0:1], 5.5), writes=["Tt0"])
+    op("v", lambda: V.memset(T.Tt[:, 0:1], 11.0), writes=["Tt0"])
     op("v", lambda: V.tensor_scalar(T.pa[:], T.pi[:], 15, None, A.bitwise_and), ["pi"], ["pa"])
     op("v", lambda: V.tensor_copy(T.pmf[:], T.pa[:]), ["pa"], ["pmf"])
-    op("v", lambda: V.tensor_scalar(T.rm[:], T.kk[:], T.pmf[:, 0:1], None, A.is_equal), ["kk", "pmf"], ["rm"])
-    op("v", lambda: V.tensor_scalar(T.wt[:], T.pmf[:], 2.0, 1.0, A.mult, A.add), ["pmf"], ["wt"])
     for a in range(16):
         op("v", lambda a=a: V.tensor_copy(T.LA[:, a * 129:(a + 1) * 128:16], T.BO[:, 0:128:16]), ["BO", "LA"] if a == 0 else ["BO"], ["LAk%d" % a])
     LA = ["LAk%d" % a for a in range(16)]
+    op("v", lambda: V.tensor_scalar(T.wt[:], T.pmf[:], 2.0, 1.0, A.mult, A.add), ["pmf"], ["wt"])
+    select(T.EK[:], T.LA[:], [[0, 16], [-1, 128]], A.is_equal, 0.0, 0, 1, LA, ["EK"])
+    select(T.CP[:], T.zerob[:], [[0, 128]], A.not_equal, 2048.0, 0, 1, ["zerob"], ["CP"])
+    select(T.CN[:], T.zerob[:], [[0, 128]], A.not_equal, -8388608.0, 0, 1, ["zerob"], ["CN"])
 
-    for nm, src, sc in (("TP", "SB", 8192.0), ("TPh", "SB", 4096.0), ("TLh", "TL", 0.5), ("BOh", "BO", 0.5), ("I1", "EQ", 1.0),
-                        ("IN1", "EQ", -1.0), ("IP", "EQ", 4096.0), ("IN4", "EQ", -4096.0)):
+    for nm, src, sc in (("TP", "SB", 8192.0), ("TPh", "SB", 4096.0), ("TLh", "TL", 0.5), ("IP", "EQ", 4096.0),
+                        ("IH", "EQ", 8388608.0), ("IHn", "EQ", -8388608.0), ("IDn", "EQ", -16777216.0), ("EQf", "EQ", 1.0), ("B2", "BO", 0.125), ("B130", "BO", 8.125)):
         op("s", lambda nm=nm, src=src, sc=sc: S.activation(T[nm][:], T[src][:], F.Copy, scale=sc), [src], [nm])
-    op("s", lambda: S.activation(T.LA2[:], T.LA[:], F.Copy, scale=0.5), LA, ["LA2"])
-    for k in range(16):
-        op("s", lambda k=k: S.activation(T.EK[:, k * 128:(k + 1) * 128], T.EQ[:], F.Copy, scale=T.rm[:, k:k + 1]), ["EQ", "rm"], ["EK%d" % k])
     op("s", lambda: S.activation(T.QW[:], T.LA[:], F.Copy, scale=T.wt[:, 0:1]), LA + ["wt"], ["QW"])
 
     def sl(name, t, w=NS):
         return T[name][:, t * w:(t + 1) * w]
 
-    XWIN = T.Xw[:, 16:WX + 16]
-
     def expand(k, t):
-        op("v", lambda: V.tensor_copy(T.Gx[:, k:4096:16], sl("G", t)), ["G%d" % t], ["Gx%d" % k])
+        src, key = (T.lin[:], "lin") if t == 0 else (sl("G", t), "G%d" % t)
+        if t > 0 and k in GX_ON_G:
+            select(T.Gx[:, k:4096:16], src, [[0, NS]], A.is_equal, 0.0, 0, 0, [key], ["Gx%d" % k])
+        else:
+            op("v", lambda: V.tensor_copy(T.Gx[:, k:4096:16], src), [key], ["Gx%d" % k])
     GX = ["Gx%d" % k for k in range(16)]
+    XIN = ["xin%d" % j for j in range(NX)] + ["xinz"]
+    X = ["X%d" % j for j in range(NX + 1)]
 
-    op("v", lambda: V.tensor_scalar(sl("G", 0), T.lin[:], 128.0, None, A.add), ["lin"], ["G0"])
     for k in range(16):
         expand(k, 0)
     op("v", lambda: V.tensor_copy(sl("UK", 0), T.gin[:]), ["gin"], ["UK0"])
     op("v", lambda: V.tensor_copy(sl("UL", 0), T.nin[:]), ["nin"], ["UL0"])
-    op("v", lambda: V.tensor_scalar(sl("KF", 0), T.gin[:], -2048.0, None, A.add), ["gin"], ["KF0"])
-    op("v", lambda: V.tensor_scalar(sl("LF", 0), T.nin[:], -2048.0, None, A.add), ["nin"], ["LF0"])
-    op("v", lambda: V.tensor_scalar(T.w0[:], T.gin[:], 4096.0, None, A.mult), ["gin"], ["w0"])
+
+    def float_lists(t):
+        op("v", lambda: V.tensor_scalar(sl("LF", t), sl("UL", t), -2048.0, None, A.add), ["UL%d" % t], ["LF%d" % t])
+        op("v", lambda: V.tensor_scalar(sl("KF", t), sl("UK", t), -2048.0, None, A.add), ["UK%d" % t], ["KF%d" % t])
     op("v", lambda: V.tensor_scalar(T.Ck[:], T.pmf[:], -4096.0, -4096.0, A.mult, A.add), ["pmf"], ["Ck"])
     op("v", lambda: V.tensor_scalar(T.zz[:], T.pmf[:], 0.0, -1.5, A.is_equal, A.mult), ["pmf"], ["zz"])
-    op("v", lambda: V.tensor_tensor(sl("Wi", 0), T.w0[:], T.nin[:], A.add), ["w0", "nin"], ["Wi0"])
+    float_lists(0)
     op("v", lambda: V.tensor_scalar(T.thr[:], T.pmf[:], 0.5, T.zz[:, 0:1], A.mult, A.add), ["pmf", "zz"], ["thr"])
-    for j in range(NX):
-        op("v", lambda j=j: V.tensor_scalar(T.Xw[:, 16 + j * xs:16 + (j + 1) * xs], T.Xin[:, j * xs:(j + 1) * xs], 128.0, None, A.add),
-           ["xin%d" % j], ["X%d" % (j + 1)])
-    X = ["X%d" % j for j in range(NX + 1)]
+    op("v", lambda: V.tensor_scalar(T.p16a[:], T.p16[:], 255, None, A.bitwise_and), ["p16"], ["p16a"])
+    fill("half", 0.5)
+    op("v", lambda: V.tensor_tensor(T.base[:], T.p16a[:], T.c256[:], A.add), ["p16a", "c256"], ["base"])
+
+    def bias(j, q):
+        out, in_ = T.Xw[:, 16 + j * xs:16 + (j + 1) * xs], T.Xin[:, 16 + j * xs:16 + (j + 1) * xs]
+        if q == "v":
+            op("v", lambda: V.tensor_scalar(out, in_, 128.0, None, A.add), ["xin%d" % j], ["X%d" % (j + 1)])
+        else:
+            op("s", lambda: S.activation(out, in_, F.Copy, bias=128.0), ["xin%d" % j], ["X%d" % (j + 1)])
 
     def release_chunk(t, c, q):
         n = RCH[c]
@@ -266,30 +280,55 @@ def rank_program(g, core, T, topo):
             op("v", lambda: V.tensor_copy(dst, T.Mw[:, 0:4096].indirect(off)), MW + ["UL%d" % t], ["RG%d" % c])
         else:
             op("s", lambda: S.activation(dst, T.Mw[:, 0:4096].indirect(off), F.Copy), MW + ["UL%d" % t], ["RG%d" % c])
+        if c in (SHIFT0 if t == 0 else SHIFT):
+            shift(t, c)
 
-    def release_pick(t, c):
+    def shift(t, c):
+        c0, w = 16 * sum(RCH[:c]), 16 * RCH[c] - 15
+        sem = "rs%d" % (t * len(RCH) + c)
+        meet("y", deps("y", ["RG%d" % c], ["RS%d" % c], ()))
+        for k in range(16):
+            g.sync.dma_start(T.RS[k:128:16, c0:c0 + w], T.RG[k:128:16, c0 + k:c0 + k + w]).then_inc(T.sem[sem], 16)
+        total[sem] = 256
+        snap[(sem, 256)] = dict(clock["y"])
+        record((sem, 256), ["RG%d" % c], ["RS%d" % c], ())
+
+    def extra(items, q):
+        for it in items:
+            if it[0] == "b":
+                bias(int(it[1:]), q)
+            else:
+                release_chunk(0, int(it[1:]), q)
+
+    def pick_open():
+        op("t", lambda: P.matmul(T.pR[:, 0:NS], T.CN[:], T.onesb[:], True, False), ["CN", "onesb"], ["pR"], ["pR"])
+
+    def pick(t, c):
         n = RCH[c]
         c0 = sum(RCH[:c])
-        o = T.pR[:, c0:c0 + n]
-        w = ["pR%d" % c]
-        op("t", lambda: P.matmul(o, T.IN4[:], T.KF[:, t * NS + c0:t * NS + c0 + n], True, False), ["IN4", "KF%d" % t], w, ["pR"])
-        op("t", lambda: P.matmul(o, T.IN1[:], T.LF[:, t * NS + c0:t * NS + c0 + n], False, False), ["IN1", "LF%d" % t], w, ["pR"])
-        op("t", lambda: P.matmul(o, T.CN[:], T.onesb[:, 0:n], False, False), ["CN", "onesb"], w, ["pR"])
+        if c in (SHIFT0 if t == 0 else SHIFT):
+            op("t", lambda: P.matmul(T.pR[:, c0:c0 + n], T.EQf[:], T.RS[:, 16 * c0:16 * (c0 + n):16], False, False), ["EQf", "RS%d" % c], ["pR"], ["pR"])
+            return
         for k in range(16):
-            op("t", lambda k=k: P.matmul(o, T.EK[:, k * 128:(k + 1) * 128], T.RG[:, 16 * c0 + k:16 * (c0 + n):16], False, k == 15),
-               ["EK%d" % k, "RG%d" % c], w, ["pR"])
+            op("t", lambda k=k: P.matmul(T.pR[:, c0:c0 + n], T.EK[:, k * 128:(k + 1) * 128], T.RG[:, 16 * c0 + k:16 * (c0 + n):16], False, False),
+               ["EK", "RG%d" % c], ["pR"], ["pR"])
 
     nch = len(CH)
     starts = [sum(CH[:c]) for c in range(nch)]
 
     for t in range(RO):
-        G, G4, H = sl("G", t), sl("G4", t), sl("H", t)
+        G = T.lin[:] if t == 0 else sl("G", t)
+        gk = "lin" if t == 0 else "G%d" % t
+        G4, H = sl("G4", t), sl("H", t)
         last = t == RO - 1
+        xbuf, xk = (T.Xin, XIN) if t == 0 else (T.Xw, X)
+        W1 = T.pF[:, NS:2 * NS]
+        xwin, xwide = xbuf[:, 16:WX + 16], xbuf[:, 0:WX + 16]
 
         def gather(c):
             a, b = starts[c], starts[c] + CH[c]
-            op("v", lambda: V.tensor_tensor(T.dd[:, 16 * a:16 * b], XWIN.indirect(T.UK[:, t * NS + a:t * NS + b]), T.Gx[:, 16 * a:16 * b], A.subtract),
-               X + GX + ["UK%d" % t], ["dd%d" % c])
+            op("v", lambda: V.tensor_tensor(T.dd[:, 16 * a:16 * b], xwin.indirect(T.UK[:, t * NS + a:t * NS + b]), T.Gx[:, 16 * a:16 * b], A.subtract),
+               xk + GX + ["UK%d" % t], ["dd%d" % c])
 
         def under(c):
             a, b = starts[c], starts[c] + CH[c]
@@ -301,46 +340,51 @@ def rank_program(g, core, T, topo):
             if c in OVER_ON_S:
                 op("s", lambda: S.activation(T.oi[:, 16 * a:16 * b], T.dd[:, 16 * a:16 * b], F.Sign, bias=-4.5, scale=1.0), ["dd%d" % c], ["oi%d" % c])
             else:
-                op("v", lambda: V.tensor_scalar(T.oi[:, 16 * a:16 * b], T.dd[:, 16 * a:16 * b], 4.0, None, A.is_gt), ["dd%d" % c], ["oi%d" % c])
+                op("v", lambda: V.tensor_scalar(T.oi[:, 16 * a:16 * b], T.dd[:, 16 * a:16 * b], 4.0, 2.0, A.is_gt, A.mult), ["dd%d" % c], ["oi%d" % c])
 
         def counts(c):
             a, n = starts[c], CH[c]
-            oo, uu = T.pO[:, a:a + n], T.pU[:, a:a + n]
-            m, mk = ("LA2", lambda k: "LA2") if c in OVER_ON_S else ("LA", lambda k: "LAk%d" % k)
+            on_s = c in OVER_ON_S
 
             def overs():
-                if c in OVER_ON_S:
-                    op("t", lambda: P.matmul(oo, T.BOh[:], T.onesb[:, 0:n], True, False), ["BOh", "onesb"], ["pO%d" % c], ["pO"])
+                oo = T.pO[:, a:a + n]
+                if on_s:
+                    op("t", lambda: P.matmul(oo, T.BO[:], T.onesb[:, 0:n], True, False), ["BO", "onesb"], ["pO%d" % c], ["pO"])
                 for k in range(16):
-                    op("t", lambda k=k: P.matmul(oo, T[m][:, k * 128:(k + 1) * 128], T.oi[:, 16 * a + k:16 * (a + n):16], k == 0 and c not in OVER_ON_S, k == 15),
-                       [mk(k), "oi%d" % c], ["pO%d" % c], ["pO"])
+                    op("t", lambda k=k: P.matmul(oo, T.LA[:, k * 128:(k + 1) * 128], T.oi[:, 16 * a + k:16 * (a + n):16], k == 0 and not on_s, k == 15),
+                       ["LAk%d" % k, "oi%d" % c], ["pO%d" % c], ["pO"])
 
             def unders():
+                uu = T.pU[:, a:a + n]
                 for k in range(16):
                     op("t", lambda k=k: P.matmul(uu, T.LA[:, k * 128:(k + 1) * 128], T.ui[:, 16 * a + k:16 * (a + n):16], k == 0, k == 15),
                        ["LAk%d" % k, "ui%d" % c], ["pU%d" % c], ["pU"])
-            if c in OVER_ON_S:
-                unders()
-                overs()
-            else:
-                overs()
-                unders()
+            for f in ((overs, unders) if c == nch - 1 else (unders, overs)):
+                f()
 
-        if t > 0:
-            for c in range(len(RCH)):
-                release_pick(t, c)
+        if t == 0:
+            extra(S0[-1], "s")
+        pick_open()
         gather(0)
         for c in range(nch):
             if c + 1 < nch:
                 gather(c + 1)
             under(c)
             over(c)
-            if c == nch - 1:
-                op("t", lambda: P.matmul(T.pK[:, 0:NS], T.I1[:], sl("KF", t), True, False), ["I1", "KF%d" % t], ["pKa"], ["pK"])
+            if t == 0:
+                extra(S0[c], "s")
+            if t > 0:
+                for r in P1[c]:
+                    pick(t, r)
+            if c == nch - 2:
+                op("t", lambda: P.matmul(T.pK[:, 0:NS], T.EQ[:], sl("KF", t), True, False), ["EQ", "KF%d" % t], ["pKa"], ["pK"])
+                op("t", lambda: P.matmul(W1, T.IP[:], sl("KF", t), True, False), ["IP", "KF%d" % t], ["pW"], ["pF"])
+                op("t", lambda: P.matmul(W1, T.EQ[:], sl("LF", t), False, False), ["EQ", "LF%d" % t], ["pW"], ["pF"])
+                op("t", lambda: P.matmul(W1, T.CP[:], T.onesb[:], False, False), ["CP", "onesb"], ["pW"], ["pF"])
             counts(c)
 
         OC, UC = ["pO%d" % c for c in range(nch)], ["pU%d" % c for c in range(nch)]
-        dead, sgn, imp = sl("dead", t), sl("sgn", t), sl("imp", t)
+        dead, sgn = sl("dead", t), sl("sgn", t)
         op("v", lambda: V.tensor_scalar(dead, T.pO[:, 0:NS], T.Tt[:, t:t + 1], None, A.is_gt), OC + ["Tt%d" % t], ["dead"], ["pO"])
         op("s", lambda: S.activation(sgn, T.pU[:, 0:NS], F.Sign, bias=-7.0), UC, ["sgn"], ["pU"])
         op("t", lambda: P.matmul(T.pK[:, 0:NS], T.TP[:], dead, False, False), ["TP", "dead"], ["pKa"], ["pK"])
@@ -354,13 +398,12 @@ def rank_program(g, core, T, topo):
                ["LAk%d" % a, "AK"], ["pA0"], ["pA"])
         op("v", lambda: V.tensor_scalar(T.pF[:, 0:NS], T.pL[:, 0:NS], T.thr[:, 0:1], None, A.is_ge), ["pL", "thr"], ["pF"], ["pL", "pF"])
         op("v", lambda: V.tensor_tensor(AL, T.pF[:, 0:NS], sl("LF", t), A.mult), ["pF", "LF%d" % t], ["AL"], ["pF"])
-        op("s", lambda: S.activation(imp, sgn, F.Relu), ["sgn"], ["imp"])
         if not last:
             op("s", lambda: S.activation(sl("junk", t), dead, F.Copy, accum_out=T.acc[:, t:t + 1]), ["dead"], ["junk", "acc"])
 
         kl, ll, ql = sl("kl", t, 16), sl("ll", t, 16), sl("ql", t, 16)
         op("v", lambda: V.tensor_scalar(kl, T.pA[:, 0:16], 33024.0, None, A.add), ["pA0"], ["kl"], ["pA"])
-        op("v", lambda: V.tensor_tensor(G4, T.Xw[:, 0:WX + 16].indirect(kl), G, A.max), X + ["kl", "G%d" % t], ["G4%d" % t])
+        op("v", lambda: V.tensor_tensor(G4, xwide.indirect(kl), G, A.max), xk + ["kl", gk], ["G4%d" % t])
         dst = T.cores[(rank + 1 + t % (n_ranks - 1)) % n_ranks]
         rid, pid, _ = topo.addr(dst)
         eng = topo.engines(core, dst)[::2]
@@ -373,35 +416,29 @@ def rank_program(g, core, T, topo):
         for a in range(16):
             op("t", lambda a=a: P.matmul(T.pB[:, 0:16], T.LA[:, a * 128:(a + 1) * 128], T.AL[:, t * NS + a:(t + 1) * NS:16], a == 0, a == 15),
                ["LAk%d" % a, "AL"], ["pB"], ["pB"])
-        op("v", lambda: V.tensor_scalar(ll, T.pB[:, 0:16], 2048.0, None, A.add), ["pB"], ["ll"], ["pB"])
-        op("v", lambda: V.tensor_tensor(T.g1[:], T.Mw[:, 0:4096].indirect(ll), sl("Wi", t), A.subtract), MW + ["ll", "Wi%d" % t], ["g1"])
         if t == 0:
-            sc = [c for c in range(len(RCH)) if c not in R0_ON_V]
-            for c in range(max(len(sc), len(R0_ON_V))):
-                for lst, q in ((sc, "s"), (R0_ON_V, "v")):
-                    if c < len(lst):
-                        release_chunk(0, lst[c], q)
-            for c in range(max(len(sc), len(R0_ON_V))):
-                for lst in (sc, R0_ON_V):
-                    if c < len(lst):
-                        release_pick(0, lst[c])
-        op("v", lambda: V.tensor_tensor(T.t2[:], T.g1[:], dead, A.mult), ["g1", "dead"], ["t2"])
-        W1 = T.pK[:, NS:2 * NS]
-        op("v", lambda: V.tensor_tensor(T.t1[:], T.pR[:, 0:NS], imp, A.mult), ["pR%d" % c for c in range(len(RCH))] + ["imp"], ["t1"], ["pR"])
-        op("t", lambda: P.matmul(W1, T.IP[:], sl("KF", t), True, False), ["IP", "KF%d" % t], ["pKb"], ["pK"])
-        op("t", lambda: P.matmul(W1, T.I1[:], sl("LF", t), False, False), ["I1", "LF%d" % t], ["pKb"], ["pK"])
-        op("t", lambda: P.matmul(W1, T.CP[:], T.onesb[:], False, False), ["CP", "onesb"], ["pKb"], ["pK"])
-        op("t", lambda: P.matmul(W1, T.EQ[:], T.t1[:], False, True), ["EQ", "t1"], ["pKb"], ["pK"])
+            extra(S0_END, "s")
+            extra(V0_END, "v")
+        for r in range(len(RCH)):
+            if t == 0 or r not in [x for v in P1.values() for x in v]:
+                pick(t, r)
+        op("t", lambda: P.matmul(T.pR[:, 0:NS], T.IH[:], sgn, False, True), ["IH", "sgn"], ["pR"], ["pR"])
+        op("t", lambda: P.matmul(W1, T.IHn[:], sgn, False, False), ["IHn", "sgn"], ["pW"], ["pF"])
+        op("t", lambda: P.matmul(W1, T.IDn[:], dead, False, True), ["IDn", "dead"], ["pW"], ["pF"])
+        op("v", lambda: V.tensor_scalar(ll, T.pB[:, 0:16], 2048.0, None, A.add), ["pB"], ["ll"], ["pB"])
+        op("v", lambda: V.tensor_tensor(T.g1[:], T.Mw[:, 0:4096].indirect(ll), dead, A.mult), MW + ["ll", "dead"], ["g1"])
+        if t == 0:
+            extra(V0_LATE, "v")
+        op("v", lambda: V.tensor_tensor(T.m1[:], T.pR[:, 0:NS], T.g1[:], A.max), ["pR", "g1"], ["m1"], ["pR"])
         if not last:
+            if t == 0:
+                fill("onesF", 1.0)
             op("t", lambda: P.matmul(T.pB[:, 32:33], T.onesF[:], T.acc[:, t:t + 1], True, True), ["onesF", "acc"], ["pBp"], ["pB"])
-            op("v", lambda: V.tensor_copy(T.ti[:, t:t + 1], T.pB[:, 32:33]), ["pBp"], ["ti"], ["pB"])
-            op("v", lambda: V.tensor_scalar(T.tj[:, t:t + 1], T.ti[:, t:t + 1], 1, None, A.bitwise_and), ["ti"], ["tj"])
-        Wn = sl("Wi", t + 1)
-        op("v", lambda: V.tensor_tensor(Wn, W1, T.t2[:], A.add), ["pKb", "t2"], ["Wi%d" % (t + 1)], ["pK"])
+        op("v", lambda: V.tensor_tensor(T.Wn[:], W1, T.m1[:], A.max), ["pW", "m1"], ["Wn"], ["pF"])
         if not last:
-            op("v", lambda: V.tensor_scalar(T.Tt[:, t + 1:t + 2], T.tj[:, t:t + 1], 5.5, None, A.add), ["tj"], ["Tt%d" % (t + 1)])
-        op("v", lambda: V.tensor_scalar(T.L32[:], Wn, 4095, None, A.bitwise_and), ["Wi%d" % (t + 1)], ["L32"])
-        op("v", lambda: V.tensor_scalar(T.K32[:], Wn, SH, None, A.logical_shift_right), ["Wi%d" % (t + 1)], ["K32"])
+            op("v", lambda: V.tensor_copy(T.ti[:, t:t + 1], T.pB[:, 32:33]), ["pBp"], ["ti"], ["pB"])
+        op("v", lambda: V.tensor_scalar(T.L32[:], T.Wn[:], 4095, None, A.bitwise_and), ["Wn"], ["L32"])
+        op("v", lambda: V.tensor_scalar(T.K32[:], T.Wn[:], SH, None, A.logical_shift_right), ["Wn"], ["K32"])
 
         if last:
             op("v", lambda: V.tensor_copy(T.ynf[:], T.L32[:]), ["L32"], ["ynf"])
@@ -417,29 +454,33 @@ def rank_program(g, core, T, topo):
         op("v", lambda: V.tensor_copy(sl("UL", t + 1), T.L32[:]), ["L32"], ["UL%d" % (t + 1)])
         for c in range(len(RCH)):
             release_chunk(t + 1, c, "s")
+        op("v", lambda: V.tensor_copy(sl("UK", t + 1), T.K32[:]), ["K32"], ["UK%d" % (t + 1)])
+        op("v", lambda: V.tensor_scalar(T.tj[:, t:t + 1], T.ti[:, t:t + 1], 1, None, A.bitwise_and), ["ti"], ["tj"])
+        float_lists(t + 1)
+        op("v", lambda: V.tensor_scalar(T.Tt[:, t + 1:t + 2], T.tj[:, t:t + 1], 2.0, 11.0, A.mult, A.add), ["tj"], ["Tt%d" % (t + 1)])
+        G4x, g4k = G4, "G4%d" % t
+        if t == 0:
+            op("v", lambda: V.tensor_scalar(T.G4b[:], G4, 128.0, None, A.add), ["G4%d" % t], ["G4b"])
+            G4x, g4k = T.G4b[:], "G4b"
 
-        fill = [lambda: op("v", lambda: V.tensor_copy(sl("UK", t + 1), T.K32[:]), ["K32"], ["UK%d" % (t + 1)]),
-                lambda: op("v", lambda: V.tensor_scalar(sl("LF", t + 1), T.L32[:], -2048.0, None, A.add), ["L32"], ["LF%d" % (t + 1)]),
-                lambda: op("v", lambda: V.tensor_scalar(sl("KF", t + 1), T.K32[:], -2048.0, None, A.add), ["K32"], ["KF%d" % (t + 1)])]
-        for k in range(16):
-            fill.append(lambda k=k: expand(k, t + 1))
+        up = 128.0 if t == 0 else 0.0
+        copies = [k for k in range(16) if k not in GX_ON_G]
 
         def filler(n):
             for _ in range(n):
-                if fill:
-                    fill.pop(0)()
-        if t == 0:
-            op("v", lambda: V.tensor_scalar(T.p16a[:], T.p16[:], 255, None, A.bitwise_and), ["p16"], ["p16a"])
-            op("v", lambda: V.memset(T.half[:], 0.5), writes=["half"])
-            op("v", lambda: V.tensor_tensor(T.base[:], T.p16a[:], T.c256[:], A.add), ["p16a", "c256"], ["base"])
+                if copies:
+                    expand(copies.pop(0), t + 1)
+        pH, b2 = T.pL[:, NS:2 * NS], "B130" if t == 0 else "B2"
+        op("t", lambda: P.matmul(pH, T[b2][:], T.onesb[:], True, False), [b2, "onesb"], ["pH"], ["pL"])
+        op("t", lambda: P.matmul(pH, T.EQ[:], H, False, True), ["EQ", "H%d" % t], ["pH"], ["pL"])
         for a in range(16):
             op("t", lambda a=a: P.matmul(T.pA[:, 16:32], T.QW[:, a * 128:(a + 1) * 128], T.H[:, t * NS + a:(t + 1) * NS:16], a == 0, a == 15),
                ["QW", "H%d" % t], ["pA1"], ["pA"])
         q1, q2, q3 = sl("q1", t, 16), sl("q2", t, 16), sl("q3", t, 16)
-        filler(2)
-        op("v", lambda: V.tensor_scalar(sl("H2", t), H, 2.0, None, A.add), ["H%d" % t], ["H2"])
-        op("v", lambda: V.tensor_scalar(sl("Hp", t), H, -0.25, None, A.add), ["H%d" % t], ["Hp"])
-        op("v", lambda: V.tensor_tensor(sl("G", t + 1), G4, sl("H2", t), A.min), ["G4%d" % t, "H2"], ["G%d" % (t + 1)])
+        op("v", lambda: V.tensor_scalar(sl("Hp", t), H, up - 0.25, None, A.add), ["H%d" % t], ["Hp"])
+        op("v", lambda: V.tensor_tensor(sl("G", t + 1), pH, G4x, A.min), [g4k, "pH"], ["G%d" % (t + 1)], ["pL"])
+        for k in GX_ON_G:
+            expand(k, t + 1)
         op("v", lambda: V.tensor_copy(q1, T.pA[:, 16:32]), ["pA1"], ["q1"], ["pA"])
         filler(1)
         op("v", lambda: V.tensor_scalar(q2, q1, 15, None, A.bitwise_and), ["q1"], ["q2"])
@@ -448,9 +489,9 @@ def rank_program(g, core, T, topo):
         filler(1)
         op("v", lambda: V.tensor_copy(ql, q3), ["q3"], ["ql"])
         filler(1)
-        op("v", lambda: V.tensor_tensor(T.yb[:], XWIN.indirect(ql), sl("Hp", t), A.add), X + ["ql", "Hp"], ["yb"])
+        op("v", lambda: V.tensor_tensor(T.yb[:], T.Xw[:, 16:WX + 16].indirect(ql), sl("Hp", t), A.add), X + ["ql", "Hp"], ["yb"])
         filler(2)
-        op("v", lambda: V.tensor_tensor(XWIN.indirect(ql), T.yb[:], T.half[:], A.mult), ["yb", "half", "ql"], X)
+        op("v", lambda: V.tensor_tensor(T.Xw[:, 16:WX + 16].indirect(ql), T.yb[:], T.half[:], A.mult), ["yb", "half", "ql"], X[1:])
         filler(99)
 
     for s in sorted(total):

from concourse.mybir import dt, AluOpType, AxisListType, ActivationFunctionType

A = AluOpType
F = ActivationFunctionType
RO, NS, WX, SH = 4, 256, 4096, 12
CH = [64, 64, 64, 64]
OVER_ON_S = (1,)
RCH = [64, 64, 64, 64]
NX = 4
NM = 4
S0 = {-1: [], 0: [], 1: [], 2: [], 3: []}
S0_END = ["r0", "r1", "r2"]
V0_END = ["r3"]
V0_LATE = ["b0", "b1", "b2", "b3"]
SHIFT0 = ()
SHIFT = (2, 3)
P1 = {0: [0, 1], 1: [], 2: [], 3: []}
GX_ON_G = (13, 14, 15)

SCRATCH = {
    "Xin": ("sbuf", [128, WX + 16], "bfloat16"),
    "Xw": ("sbuf", [128, WX + 16], "bfloat16"),
    "Mw": ("sbuf", [128, 4096], "int32"),
    "RG": ("sbuf", [128, 4096], "float32"),
    "RS": ("sbuf", [128, 4096], "float32"),
    "EQf": ("sbuf", [128, 128], "float32"),
    "Gx": ("sbuf", [128, 4096], "bfloat16"),
    "dd": ("sbuf", [128, 4096], "bfloat16"),
    "oi": ("sbuf", [128, 4096], "bfloat16"),
    "ui": ("sbuf", [128, 4096], "bfloat16"),
    "LA": ("sbuf", [128, 2048], "bfloat16"),
    "QW": ("sbuf", [128, 2048], "bfloat16"),
    "EK": ("sbuf", [128, 2048], "float32"),
    "onesb": ("sbuf", [128, 256], "bfloat16"),
    "zerob": ("sbuf", [128, 128], "bfloat16"),
    "onesF": ("sbuf", [128, 128], "float32"),
    "half": ("sbuf", [128, 256], "bfloat16"),
    "BO": ("sbuf", [128, 128], "bfloat16"),
    "TL": ("sbuf", [128, 128], "bfloat16"),
    "TLh": ("sbuf", [128, 128], "bfloat16"),
    "SB": ("sbuf", [128, 128], "bfloat16"),
    "TP": ("sbuf", [128, 128], "bfloat16"),
    "TPh": ("sbuf", [128, 128], "bfloat16"),
    "EQ": ("sbuf", [128, 128], "bfloat16"),
    "IP": ("sbuf", [128, 128], "bfloat16"),
    "IH": ("sbuf", [128, 128], "bfloat16"),
    "IHn": ("sbuf", [128, 128], "bfloat16"),
    "IDn": ("sbuf", [128, 128], "bfloat16"),
    "CP": ("sbuf", [128, 128], "bfloat16"),
    "CN": ("sbuf", [128, 128], "bfloat16"),
    "B2": ("sbuf", [128, 128], "bfloat16"),
    "B130": ("sbuf", [128, 128], "bfloat16"),
    "pi": ("sbuf", [128, 1], "int32"),
    "pa": ("sbuf", [128, 1], "int32"),
    "pmf": ("sbuf", [128, 1], "float32"),
    "wt": ("sbuf", [128, 1], "float32"),
    "Ck": ("sbuf", [128, 1], "float32"),
    "zz": ("sbuf", [128, 1], "float32"),
    "thr": ("sbuf", [128, 1], "float32"),
    "c256": ("sbuf", [128, 16], "int32"),
    "p16": ("sbuf", [128, 16], "int32"),
    "p16a": ("sbuf", [128, 16], "int32"),
    "base": ("sbuf", [128, 16], "int32"),
    "nin": ("sbuf", [128, 256], "int32"),
    "gin": ("sbuf", [128, 256], "int32"),
    "lin": ("sbuf", [128, 256], "bfloat16"),
    "UK": ("sbuf", [128, 1024], "uint16"),
    "UL": ("sbuf", [128, 1024], "uint16"),
    "KF": ("sbuf", [128, 1024], "float16"),
    "LF": ("sbuf", [128, 1024], "float16"),
    "Wn": ("sbuf", [128, 256], "int32"),
    "G": ("sbuf", [128, 1280], "bfloat16"),
    "G4": ("sbuf", [128, 1024], "bfloat16"),
    "G4b": ("sbuf", [128, 256], "bfloat16"),
    "H": ("sbuf", [128, 1024], "bfloat16"),
    "H2": ("sbuf", [128, 1024], "bfloat16"),
    "Hp": ("sbuf", [128, 1024], "float32"),
    "dead": ("sbuf", [128, 1024], "bfloat16"),
    "sgn": ("sbuf", [128, 1024], "bfloat16"),
    "junk": ("sbuf", [128, 1024], "bfloat16"),
    "acc": ("sbuf", [128, 4], "float32"),
    "Tt": ("sbuf", [128, 4], "float32"),
    "ti": ("sbuf", [128, 4], "int32"),
    "tj": ("sbuf", [128, 4], "int32"),
    "AK": ("sbuf", [128, 1024], "float16"),
    "AL": ("sbuf", [128, 1024], "float16"),
    "kl": ("sbuf", [128, 64], "uint16"),
    "ll": ("sbuf", [128, 64], "uint16"),
    "ql": ("sbuf", [128, 64], "uint16"),
    "q1": ("sbuf", [128, 64], "int32"),
    "q2": ("sbuf", [128, 64], "int32"),
    "q3": ("sbuf", [128, 64], "int32"),
    "yb": ("sbuf", [128, 256], "bfloat16"),
    "g1": ("sbuf", [128, 256], "float32"),
    "m1": ("sbuf", [128, 256], "float32"),
    "L32": ("sbuf", [128, 256], "int32"),
    "K32": ("sbuf", [128, 256], "int32"),
    "ynf": ("sbuf", [128, 256], "float32"),
    "ygf": ("sbuf", [128, 256], "float32"),
    "ylb": ("sbuf", [128, 256], "bfloat16"),
    "gsh": ("sbuf", [128, 256], "bfloat16"),
    "pO": ("psum", [128, 512], "float32"),
    "pU": ("psum", [128, 512], "float32"),
    "pK": ("psum", [128, 512], "float32"),
    "pL": ("psum", [128, 512], "float32"),
    "pF": ("psum", [128, 512], "float32"),
    "pA": ("psum", [128, 512], "float32"),
    "pB": ("psum", [128, 512], "float32"),
    "pR": ("psum", [128, 512], "float32"),
}
SEMAPHORES = (["cv", "cs", "ct", "cg", "dn", "dg", "dl", "on", "og", "ol"] + ["dx%d" % j for j in range(NX)]
              + ["dm%d" % j for j in range(NM)] + ["arr%d" % t for t in range(RO)] + ["loc%d" % t for t in range(RO)] + ["rs%d" % j for j in range(RO * len(RCH))])


def rank_program(g, core, T, topo):
    rank = T.rank_of(core)
    if rank is None:
        return
    n_ranks = len(T.cores)
    queue = {"v": g.vector, "s": g.scalar, "t": g.tensor, "g": g, "y": g.sync}
    count = {"v": 0, "s": 0, "t": 0, "g": 0}
    clock = {q: {} for q in queue}
    snap = {}
    last_w, readers, bank_acc, total = {}, {}, {}, {}

    def meet(q, needs):
        for s in sorted(needs):
            v = needs[s]
            if clock[q].get(s, 0) >= v:
                continue
            queue[q].wait_ge(T.sem[s], v)
            for s2, v2 in snap.get((s, v), {}).items():
                if clock[q].get(s2, 0) < v2:
                    clock[q][s2] = v2
            clock[q][s] = v

    def deps(q, reads, writes, banks):
        own = "c" + q
        needs = {}

        def add(ev):
            if ev[1] > needs.get(ev[0], 0):
                needs[ev[0]] = ev[1]
        for r in reads:
            if r in last_w:
                add(last_w[r])
        for w in writes:
            if w in last_w and not (q == "t" and last_w[w][0] == own):
                add(last_w[w])
            for s, v in readers.get(w, {}).items():
                if s != own:
                    add((s, v))
        for b in banks:
            for s, v in bank_acc.get(b, {}).items():
                if s != own:
                    add((s, v))
        return needs

    def record(ev, reads, writes, banks):
        for r in reads:
            d = readers.setdefault(r, {})
            d[ev[0]] = max(d.get(ev[0], 0), ev[1])
        for w in writes:
            last_w[w] = ev
            readers[w] = {}
        for b in banks:
            bank_acc.setdefault(b, {})[ev[0]] = ev[1]

    def op(q, fn, reads=(), writes=(), banks=()):
        meet(q, deps(q, reads, writes, banks))
        ins = fn()
        count[q] += 1
        ev = ("c" + q, count[q])
        ins.then_inc(T.sem[ev[0]], 1)
        total[ev[0]] = count[q]
        snap[ev] = dict(clock[q])
        record(ev, reads, writes, banks)

    def dma(q, sem, out, in_, reads=(), writes=()):
        meet(q, deps(q, reads, writes, ()))
        queue[q].dma_start(out, in_).then_inc(T.sem[sem], 16)
        ev = (sem, 16)
        total[sem] = 16
        snap[ev] = dict(clock[q])
        record(ev, reads, writes, ())

    V, S, P = g.vector, g.scalar, g.tensor

    xs = WX // NX
    ms = 4096 // NM
    dma("s", "dl", T.lin[:], T.lim[:], writes=["lin"])
    dma("y", "dg", T.gin[:], T.grd[:], writes=["gin"])
    dma("s", "dn", T.nin[:], T.nam[:], writes=["nin"])
    for j in range(NX):
        dma("y", "dx%d" % j, T.Xin[:, 16 + j * xs:16 + (j + 1) * xs], T.xc[:, j * xs:(j + 1) * xs], writes=["xin%d" % j])
    for j in range(NM):
        dma("y", "dm%d" % j, T.Mw[:, j * ms:(j + 1) * ms], T.rel[:, j * ms:(j + 1) * ms], writes=["mw%d" % j])
    MW = ["mw%d" % j for j in range(NM)]

    def fill(name, val):
        op("v", lambda: V.memset(T[name][:], val), writes=[name])

    def select(out, in_, pattern, cmp, val, base, mult, reads, writes):
        op("g", lambda: g.affine_select(out, in_, pattern, cmp, val, base, mult), reads, writes)

    fill("onesb", 1.0)
    fill("zerob", 0.0)
    select(T.BO[:], T.onesb[:, 0:128], [[-16, 8], [0, 16]], A.is_ge, 0.0, 0, 1, ["onesb"], ["BO"])
    select(T.BO[:], T.BO[:], [[16, 8], [0, 16]], A.is_ge, 0.0, 15, -1, ["BO"], ["BO"])
    op("g", lambda: g.iota(T.pi[:], [[0, 1]], 0, 1), writes=["pi"])
    op("g", lambda: g.iota(T.c256[:], [[256, 16]], 0, 0), writes=["c256"])
    op("g", lambda: g.iota(T.p16[:], [[0, 16]], 0, 16), writes=["p16"])
    select(T.EQ[:], T.onesb[:, 0:128], [[-1, 128]], A.is_equal, 0.0, 0, 1, ["onesb"], ["EQ"])
    select(T.SB[:], T.BO[:], [[1, 128]], A.is_gt, 0.0, 0, -1, ["BO"], ["SB"])
    select(T.SB[:], T.SB[:], [[1, 128]], A.not_equal, -1.0, 0, -1, ["SB"], ["SB"])
    select(T.TL[:], T.SB[:], [[0, 128]], A.is_equal, 0.0, 0, 0, ["SB"], ["TL"])
    select(T.TL[:, 0:128:16], T.BO[:, 0:128:16], [[16, 8]], A.not_equal, -17.0, 0, -1, ["BO", "TL"], ["TL"])

    fill("LA", 0.0)
    op("v", lambda: V.memset(T.Xin[:, 0:16], 0.0), writes=["xinz"])
    op("v", lambda: V.memset(T.Xw[:, 0:16], 0.0), writes=["X0"])
    op("v", lambda: V.memset(T.Tt[:, 0:1], 11.0), writes=["Tt0"])
    op("v", lambda: V.tensor_scalar(T.pa[:], T.pi[:], 15, None, A.bitwise_and), ["pi"], ["pa"])
    op("v", lambda: V.tensor_copy(T.pmf[:], T.pa[:]), ["pa"], ["pmf"])
    for a in range(16):
        op("v", lambda a=a: V.tensor_copy(T.LA[:, a * 129:(a + 1) * 128:16], T.BO[:, 0:128:16]), ["BO", "LA"] if a == 0 else ["BO"], ["LAk%d" % a])
    LA = ["LAk%d" % a for a in range(16)]
    op("v", lambda: V.tensor_scalar(T.wt[:], T.pmf[:], 2.0, 1.0, A.mult, A.add), ["pmf"], ["wt"])
    select(T.EK[:], T.LA[:], [[0, 16], [-1, 128]], A.is_equal, 0.0, 0, 1, LA, ["EK"])
    select(T.CP[:], T.zerob[:], [[0, 128]], A.not_equal, 2048.0, 0, 1, ["zerob"], ["CP"])
    select(T.CN[:], T.zerob[:], [[0, 128]], A.not_equal, -8388608.0, 0, 1, ["zerob"], ["CN"])

    for nm, src, sc in (("TP", "SB", 8192.0), ("TPh", "SB", 4096.0), ("TLh", "TL", 0.5), ("IP", "EQ", 4096.0),
                        ("IH", "EQ", 8388608.0), ("IHn", "EQ", -8388608.0), ("IDn", "EQ", -16777216.0), ("EQf", "EQ", 1.0), ("B2", "BO", 0.125), ("B130", "BO", 8.125)):
        op("s", lambda nm=nm, src=src, sc=sc: S.activation(T[nm][:], T[src][:], F.Copy, scale=sc), [src], [nm])
    op("s", lambda: S.activation(T.QW[:], T.LA[:], F.Copy, scale=T.wt[:, 0:1]), LA + ["wt"], ["QW"])

    def sl(name, t, w=NS):
        return T[name][:, t * w:(t + 1) * w]

    def expand(k, t):
        src, key = (T.lin[:], "lin") if t == 0 else (sl("G", t), "G%d" % t)
        if t > 0 and k in GX_ON_G:
            select(T.Gx[:, k:4096:16], src, [[0, NS]], A.is_equal, 0.0, 0, 0, [key], ["Gx%d" % k])
        else:
            op("v", lambda: V.tensor_copy(T.Gx[:, k:4096:16], src), [key], ["Gx%d" % k])
    GX = ["Gx%d" % k for k in range(16)]
    XIN = ["xin%d" % j for j in range(NX)] + ["xinz"]
    X = ["X%d" % j for j in range(NX + 1)]

    for k in range(16):
        expand(k, 0)
    op("v", lambda: V.tensor_copy(sl("UK", 0), T.gin[:]), ["gin"], ["UK0"])
    op("v", lambda: V.tensor_copy(sl("UL", 0), T.nin[:]), ["nin"], ["UL0"])

    def float_lists(t):
        op("v", lambda: V.tensor_scalar(sl("LF", t), sl("UL", t), -2048.0, None, A.add), ["UL%d" % t], ["LF%d" % t])
        op("v", lambda: V.tensor_scalar(sl("KF", t), sl("UK", t), -2048.0, None, A.add), ["UK%d" % t], ["KF%d" % t])
    op("v", lambda: V.tensor_scalar(T.Ck[:], T.pmf[:], -4096.0, -4096.0, A.mult, A.add), ["pmf"], ["Ck"])
    op("v", lambda: V.tensor_scalar(T.zz[:], T.pmf[:], 0.0, -1.5, A.is_equal, A.mult), ["pmf"], ["zz"])
    float_lists(0)
    op("v", lambda: V.tensor_scalar(T.thr[:], T.pmf[:], 0.5, T.zz[:, 0:1], A.mult, A.add), ["pmf", "zz"], ["thr"])
    op("v", lambda: V.tensor_scalar(T.p16a[:], T.p16[:], 255, None, A.bitwise_and), ["p16"], ["p16a"])
    fill("half", 0.5)
    op("v", lambda: V.tensor_tensor(T.base[:], T.p16a[:], T.c256[:], A.add), ["p16a", "c256"], ["base"])

    def bias(j, q):
        out, in_ = T.Xw[:, 16 + j * xs:16 + (j + 1) * xs], T.Xin[:, 16 + j * xs:16 + (j + 1) * xs]
        if q == "v":
            op("v", lambda: V.tensor_scalar(out, in_, 128.0, None, A.add), ["xin%d" % j], ["X%d" % (j + 1)])
        else:
            op("s", lambda: S.activation(out, in_, F.Copy, bias=128.0), ["xin%d" % j], ["X%d" % (j + 1)])

    def release_chunk(t, c, q):
        n = RCH[c]
        c0 = sum(RCH[:c])
        off = T.UL[:, t * NS + c0:t * NS + c0 + n]
        dst = T.RG[:, 16 * c0:16 * (c0 + n)]
        if q == "v":
            op("v", lambda: V.tensor_copy(dst, T.Mw[:, 0:4096].indirect(off)), MW + ["UL%d" % t], ["RG%d" % c])
        else:
            op("s", lambda: S.activation(dst, T.Mw[:, 0:4096].indirect(off), F.Copy), MW + ["UL%d" % t], ["RG%d" % c])
        if c in (SHIFT0 if t == 0 else SHIFT):
            shift(t, c)

    def shift(t, c):
        c0, w = 16 * sum(RCH[:c]), 16 * RCH[c] - 15
        sem = "rs%d" % (t * len(RCH) + c)
        meet("y", deps("y", ["RG%d" % c], ["RS%d" % c], ()))
        for k in range(16):
            g.sync.dma_start(T.RS[k:128:16, c0:c0 + w], T.RG[k:128:16, c0 + k:c0 + k + w]).then_inc(T.sem[sem], 16)
        total[sem] = 256
        snap[(sem, 256)] = dict(clock["y"])
        record((sem, 256), ["RG%d" % c], ["RS%d" % c], ())

    def extra(items, q):
        for it in items:
            if it[0] == "b":
                bias(int(it[1:]), q)
            else:
                release_chunk(0, int(it[1:]), q)

    def pick_open():
        op("t", lambda: P.matmul(T.pR[:, 0:NS], T.CN[:], T.onesb[:], True, False), ["CN", "onesb"], ["pR"], ["pR"])

    def pick(t, c):
        n = RCH[c]
        c0 = sum(RCH[:c])
        if c in (SHIFT0 if t == 0 else SHIFT):
            op("t", lambda: P.matmul(T.pR[:, c0:c0 + n], T.EQf[:], T.RS[:, 16 * c0:16 * (c0 + n):16], False, False), ["EQf", "RS%d" % c], ["pR"], ["pR"])
            return
        for k in range(16):
            op("t", lambda k=k: P.matmul(T.pR[:, c0:c0 + n], T.EK[:, k * 128:(k + 1) * 128], T.RG[:, 16 * c0 + k:16 * (c0 + n):16], False, False),
               ["EK", "RG%d" % c], ["pR"], ["pR"])

    nch = len(CH)
    starts = [sum(CH[:c]) for c in range(nch)]

    for t in range(RO):
        G = T.lin[:] if t == 0 else sl("G", t)
        gk = "lin" if t == 0 else "G%d" % t
        G4, H = sl("G4", t), sl("H", t)
        last = t == RO - 1
        xbuf, xk = (T.Xin, XIN) if t == 0 else (T.Xw, X)
        W1 = T.pF[:, NS:2 * NS]
        xwin, xwide = xbuf[:, 16:WX + 16], xbuf[:, 0:WX + 16]

        def gather(c):
            a, b = starts[c], starts[c] + CH[c]
            op("v", lambda: V.tensor_tensor(T.dd[:, 16 * a:16 * b], xwin.indirect(T.UK[:, t * NS + a:t * NS + b]), T.Gx[:, 16 * a:16 * b], A.subtract),
               xk + GX + ["UK%d" % t], ["dd%d" % c])

        def under(c):
            a, b = starts[c], starts[c] + CH[c]
            op("s", lambda: S.activation(T.ui[:, 16 * a:16 * b], T.dd[:, 16 * a:16 * b], F.Sign, bias=0.5, scale=-1.0),
               ["dd%d" % c], ["ui%d" % c])

        def over(c):
            a, b = starts[c], starts[c] + CH[c]
            if c in OVER_ON_S:
                op("s", lambda: S.activation(T.oi[:, 16 * a:16 * b], T.dd[:, 16 * a:16 * b], F.Sign, bias=-4.5, scale=1.0), ["dd%d" % c], ["oi%d" % c])
            else:
                op("v", lambda: V.tensor_scalar(T.oi[:, 16 * a:16 * b], T.dd[:, 16 * a:16 * b], 4.0, 2.0, A.is_gt, A.mult), ["dd%d" % c], ["oi%d" % c])

        def counts(c):
            a, n = starts[c], CH[c]
            on_s = c in OVER_ON_S

            def overs():
                oo = T.pO[:, a:a + n]
                if on_s:
                    op("t", lambda: P.matmul(oo, T.BO[:], T.onesb[:, 0:n], True, False), ["BO", "onesb"], ["pO%d" % c], ["pO"])
                for k in range(16):
                    op("t", lambda k=k: P.matmul(oo, T.LA[:, k * 128:(k + 1) * 128], T.oi[:, 16 * a + k:16 * (a + n):16], k == 0 and not on_s, k == 15),
                       ["LAk%d" % k, "oi%d" % c], ["pO%d" % c], ["pO"])

            def unders():
                uu = T.pU[:, a:a + n]
                for k in range(16):
                    op("t", lambda k=k: P.matmul(uu, T.LA[:, k * 128:(k + 1) * 128], T.ui[:, 16 * a + k:16 * (a + n):16], k == 0, k == 15),
                       ["LAk%d" % k, "ui%d" % c], ["pU%d" % c], ["pU"])
            for f in ((overs, unders) if c == nch - 1 else (unders, overs)):
                f()

        if t == 0:
            extra(S0[-1], "s")
        pick_open()
        gather(0)
        for c in range(nch):
            if c + 1 < nch:
                gather(c + 1)
            under(c)
            over(c)
            if t == 0:
                extra(S0[c], "s")
            if t > 0:
                for r in P1[c]:
                    pick(t, r)
            if c == nch - 2:
                op("t", lambda: P.matmul(T.pK[:, 0:NS], T.EQ[:], sl("KF", t), True, False), ["EQ", "KF%d" % t], ["pKa"], ["pK"])
                op("t", lambda: P.matmul(W1, T.IP[:], sl("KF", t), True, False), ["IP", "KF%d" % t], ["pW"], ["pF"])
                op("t", lambda: P.matmul(W1, T.EQ[:], sl("LF", t), False, False), ["EQ", "LF%d" % t], ["pW"], ["pF"])
                op("t", lambda: P.matmul(W1, T.CP[:], T.onesb[:], False, False), ["CP", "onesb"], ["pW"], ["pF"])
            counts(c)

        OC, UC = ["pO%d" % c for c in range(nch)], ["pU%d" % c for c in range(nch)]
        dead, sgn = sl("dead", t), sl("sgn", t)
        op("v", lambda: V.tensor_scalar(dead, T.pO[:, 0:NS], T.Tt[:, t:t + 1], None, A.is_gt), OC + ["Tt%d" % t], ["dead"], ["pO"])
        op("s", lambda: S.activation(sgn, T.pU[:, 0:NS], F.Sign, bias=-7.0), UC, ["sgn"], ["pU"])
        op("t", lambda: P.matmul(T.pK[:, 0:NS], T.TP[:], dead, False, False), ["TP", "dead"], ["pKa"], ["pK"])
        op("t", lambda: P.matmul(T.pK[:, 0:NS], T.TPh[:], sgn, False, True), ["TPh", "sgn"], ["pKa"], ["pK"])
        op("t", lambda: P.matmul(T.pL[:, 0:NS], T.TL[:], dead, True, False), ["TL", "dead"], ["pL"], ["pL"])
        op("t", lambda: P.matmul(T.pL[:, 0:NS], T.TLh[:], sgn, False, True), ["TLh", "sgn"], ["pL"], ["pL"])
        AK, AL = sl("AK", t), sl("AL", t)
        op("v", lambda: V.tensor_scalar(AK, T.pK[:, 0:NS], T.Ck[:, 0:1], -2064.0, A.add, A.max), ["pKa", "Ck"], ["AK"], ["pK"])
        for a in range(16):
            op("t", lambda a=a: P.matmul(T.pA[:, 0:16], T.LA[:, a * 128:(a + 1) * 128], T.AK[:, t * NS + a:(t + 1) * NS:16], a == 0, a == 15),
               ["LAk%d" % a, "AK"], ["pA0"], ["pA"])
        op("v", lambda: V.tensor_scalar(T.pF[:, 0:NS], T.pL[:, 0:NS], T.thr[:, 0:1], None, A.is_ge), ["pL", "thr"], ["pF"], ["pL", "pF"])
        op("v", lambda: V.tensor_tensor(AL, T.pF[:, 0:NS], sl("LF", t), A.mult), ["pF", "LF%d" % t], ["AL"], ["pF"])
        if not last:
            op("s", lambda: S.activation(sl("junk", t), dead, F.Copy, accum_out=T.acc[:, t:t + 1]), ["dead"], ["junk", "acc"])

        kl, ll, ql = sl("kl", t, 16), sl("ll", t, 16), sl("ql", t, 16)
        op("v", lambda: V.tensor_scalar(kl, T.pA[:, 0:16], 33024.0, None, A.add), ["pA0"], ["kl"], ["pA"])
        op("v", lambda: V.tensor_tensor(G4, xwide.indirect(kl), G, A.max), xk + ["kl", gk], ["G4%d" % t])
        dst = T.cores[(rank + 1 + t % (n_ranks - 1)) % n_ranks]
        rid, pid, _ = topo.addr(dst)
        eng = topo.engines(core, dst)[::2]
        meet("g", deps("g", ["G4%d" % t], [], ()))
        g.remote_dma(H, G4, T.sem["arr%d" % t], T.sem["loc%d" % t], pid, rid, sum(1 << e for e in eng))
        total["arr%d" % t] = len(eng)
        total["loc%d" % t] = len(eng)
        last_w["H%d" % t] = ("arr%d" % t, len(eng))

        for a in range(16):
            op("t", lambda a=a: P.matmul(T.pB[:, 0:16], T.LA[:, a * 128:(a + 1) * 128], T.AL[:, t * NS + a:(t + 1) * NS:16], a == 0, a == 15),
               ["LAk%d" % a, "AL"], ["pB"], ["pB"])
        if t == 0:
            extra(S0_END, "s")
            extra(V0_END, "v")
        for r in range(len(RCH)):
            if t == 0 or r not in [x for v in P1.values() for x in v]:
                pick(t, r)
        op("t", lambda: P.matmul(T.pR[:, 0:NS], T.IH[:], sgn, False, True), ["IH", "sgn"], ["pR"], ["pR"])
        op("t", lambda: P.matmul(W1, T.IHn[:], sgn, False, False), ["IHn", "sgn"], ["pW"], ["pF"])
        op("t", lambda: P.matmul(W1, T.IDn[:], dead, False, True), ["IDn", "dead"], ["pW"], ["pF"])
        op("v", lambda: V.tensor_scalar(ll, T.pB[:, 0:16], 2048.0, None, A.add), ["pB"], ["ll"], ["pB"])
        op("v", lambda: V.tensor_tensor(T.g1[:], T.Mw[:, 0:4096].indirect(ll), dead, A.mult), MW + ["ll", "dead"], ["g1"])
        if t == 0:
            extra(V0_LATE, "v")
        op("v", lambda: V.tensor_tensor(T.m1[:], T.pR[:, 0:NS], T.g1[:], A.max), ["pR", "g1"], ["m1"], ["pR"])
        if not last:
            if t == 0:
                fill("onesF", 1.0)
            op("t", lambda: P.matmul(T.pB[:, 32:33], T.onesF[:], T.acc[:, t:t + 1], True, True), ["onesF", "acc"], ["pBp"], ["pB"])
        op("v", lambda: V.tensor_tensor(T.Wn[:], W1, T.m1[:], A.max), ["pW", "m1"], ["Wn"], ["pF"])
        if not last:
            op("v", lambda: V.tensor_copy(T.ti[:, t:t + 1], T.pB[:, 32:33]), ["pBp"], ["ti"], ["pB"])
        op("v", lambda: V.tensor_scalar(T.L32[:], T.Wn[:], 4095, None, A.bitwise_and), ["Wn"], ["L32"])
        op("v", lambda: V.tensor_scalar(T.K32[:], T.Wn[:], SH, None, A.logical_shift_right), ["Wn"], ["K32"])

        if last:
            op("v", lambda: V.tensor_copy(T.ynf[:], T.L32[:]), ["L32"], ["ynf"])
            dma("y", "on", T.yn[:], T.ynf[:], ["ynf"])
            op("v", lambda: V.tensor_copy(T.ygf[:], T.K32[:]), ["K32"], ["ygf"])
            dma("s", "og", T.yg[:], T.ygf[:], ["ygf"])
            op("v", lambda: V.tensor_scalar(T.gsh[:], G4, -128.0, None, A.add), ["G4%d" % t], ["gsh"])
            op("v", lambda: V.tensor_scalar(sl("H2", t), H, -126.0, None, A.add), ["H%d" % t], ["H2"])
            op("v", lambda: V.tensor_tensor(T.ylb[:], T.gsh[:], sl("H2", t), A.min), ["gsh", "H2"], ["ylb"])
            dma("y", "ol", T.yl[:], T.ylb[:], ["ylb"])
            break

        op("v", lambda: V.tensor_copy(sl("UL", t + 1), T.L32[:]), ["L32"], ["UL%d" % (t + 1)])
        for c in range(len(RCH)):
            release_chunk(t + 1, c, "s")
        op("v", lambda: V.tensor_copy(sl("UK", t + 1), T.K32[:]), ["K32"], ["UK%d" % (t + 1)])
        op("v", lambda: V.tensor_scalar(T.tj[:, t:t + 1], T.ti[:, t:t + 1], 1, None, A.bitwise_and), ["ti"], ["tj"])
        float_lists(t + 1)
        op("v", lambda: V.tensor_scalar(T.Tt[:, t + 1:t + 2], T.tj[:, t:t + 1], 2.0, 11.0, A.mult, A.add), ["tj"], ["Tt%d" % (t + 1)])
        G4x, g4k = G4, "G4%d" % t
        if t == 0:
            op("v", lambda: V.tensor_scalar(T.G4b[:], G4, 128.0, None, A.add), ["G4%d" % t], ["G4b"])
            G4x, g4k = T.G4b[:], "G4b"

        up = 128.0 if t == 0 else 0.0
        copies = [k for k in range(16) if k not in GX_ON_G]

        def filler(n):
            for _ in range(n):
                if copies:
                    expand(copies.pop(0), t + 1)
        pH, b2 = T.pL[:, NS:2 * NS], "B130" if t == 0 else "B2"
        op("t", lambda: P.matmul(pH, T[b2][:], T.onesb[:], True, False), [b2, "onesb"], ["pH"], ["pL"])
        op("t", lambda: P.matmul(pH, T.EQ[:], H, False, True), ["EQ", "H%d" % t], ["pH"], ["pL"])
        for a in range(16):
            op("t", lambda a=a: P.matmul(T.pA[:, 16:32], T.QW[:, a * 128:(a + 1) * 128], T.H[:, t * NS + a:(t + 1) * NS:16], a == 0, a == 15),
               ["QW", "H%d" % t], ["pA1"], ["pA"])
        q1, q2, q3 = sl("q1", t, 16), sl("q2", t, 16), sl("q3", t, 16)
        op("v", lambda: V.tensor_scalar(sl("Hp", t), H, up - 0.25, None, A.add), ["H%d" % t], ["Hp"])
        op("v", lambda: V.tensor_tensor(sl("G", t + 1), pH, G4x, A.min), [g4k, "pH"], ["G%d" % (t + 1)], ["pL"])
        for k in GX_ON_G:
            expand(k, t + 1)
        op("v", lambda: V.tensor_copy(q1, T.pA[:, 16:32]), ["pA1"], ["q1"], ["pA"])
        filler(1)
        op("v", lambda: V.tensor_scalar(q2, q1, 15, None, A.bitwise_and), ["q1"], ["q2"])
        filler(1)
        op("v", lambda: V.tensor_tensor(q3, q2, T.base[:], A.add), ["q2", "base"], ["q3"])
        filler(1)
        op("v", lambda: V.tensor_copy(ql, q3), ["q3"], ["ql"])
        filler(1)
        op("v", lambda: V.tensor_tensor(T.yb[:], T.Xw[:, 16:WX + 16].indirect(ql), sl("Hp", t), A.add), X + ["ql", "Hp"], ["yb"])
        filler(2)
        op("v", lambda: V.tensor_tensor(T.Xw[:, 16:WX + 16].indirect(ql), T.yb[:], T.half[:], A.mult), ["yb", "half", "ql"], X[1:])
        filler(99)

    for s in sorted(total):
        meet("g", {s: total[s]})
